import numpy as np
import ml_dtypes


def mxq(x, axis, fmt="e4m3"):
    dtype, down = {"e4m3": (ml_dtypes.float8_e4m3fn, 7), "e5m2": (ml_dtypes.float8_e5m2, 14)}[fmt]
    v = np.moveaxis(np.asarray(x, np.float32).astype(ml_dtypes.bfloat16).astype(np.float64), axis, -1)
    blocks = v.reshape(v.shape[:-1] + (-1, 32))
    amax = np.abs(blocks).max(-1, keepdims=True)
    byte = np.maximum(np.where(amax > 0, np.frexp(amax)[1] - 1 + 127, 0) - down, 1)
    scale = np.exp2(byte - 127.0)
    codes = (blocks / scale).astype(np.float32).astype(dtype).astype(np.float64)
    return np.moveaxis((codes * scale).reshape(v.shape), -1, axis)


WIDE = False


def mx_kscale(k):
    if not WIDE:
        return np.ones(k)
    levels = np.array([10, -10, 5, -5, 0])
    if k % 512:
        return np.exp2(np.random.permutation(np.resize(levels, k // 32))).repeat(32)
    a = np.empty((k // 512, 16))
    for p in range(k // 512):
        a[p, :8] = np.random.permutation(np.resize(levels, 8))
        for g in range(8):
            far = levels[np.abs(levels - a[p, g]) >= 10]
            a[p, g + 8] = far[np.random.randint(len(far))]
    return np.exp2(a.ravel()).repeat(32)


def f64(x):
    return np.asarray(x).astype(np.float64)


def striped(idx):
    return np.tile(idx.reshape(-1, 16).T, (8, 1)).astype(np.uint16)


def unstriped(offs):
    return offs[:16].T.reshape(-1).astype(np.int64)


E2M1 = np.array([0.0, 0.5, 1.0, 1.5, 2.0, 3.0, 4.0, 6.0, -0.0, -0.5, -1.0, -1.5, -2.0, -3.0, -4.0, -6.0])


def pack_weight(w, fmt):
    k, n = w.shape
    w = f64(np.asarray(w, np.float32).astype(ml_dtypes.bfloat16)).reshape(k // 32, 32, n)
    amax = np.abs(w).max(1)
    if fmt == "e4m3":
        byte = np.frexp(amax)[1] - 1 + 127 - 7
    else:
        mant, ex = np.frexp(amax / 6.0)
        byte = np.where(mant > 0.5, ex, ex - 1) + 127
    byte = np.clip(np.where(amax > 0, byte, 1), 1, 254)
    scaled = (w * np.exp2(127.0 - byte)[:, None, :]).reshape(k, n).astype(np.float32)
    by_word = np.ascontiguousarray(scaled.reshape(k // 512, 128, 4, n).transpose(0, 1, 3, 2))
    if fmt == "e4m3":
        words = by_word.astype(ml_dtypes.float8_e4m3fn).view(np.uint8)
    else:
        c = by_word.astype(ml_dtypes.float4_e2m1fn).view(np.uint8) & 0xF
        words = (c[..., 0::2] | (c[..., 1::2] << 4)).reshape(k // 512, 128, 2 * n)
    return np.ascontiguousarray(words), np.ascontiguousarray(byte.astype(np.uint8).reshape(k // 512, 16, n))


def unpack_weight(words, scales, fmt):
    g, _, n = scales.shape
    words = np.ascontiguousarray(words).reshape(g, 128, n, -1)
    if fmt == "e4m3":
        vals = words.view(ml_dtypes.float8_e4m3fn).astype(np.float64)
    else:
        nib = np.empty((g, 128, n, 4), np.uint8)
        nib[..., 0::2] = words & 0xF
        nib[..., 1::2] = words >> 4
        vals = E2M1[nib]
    vals = vals * np.repeat(np.exp2(scales.astype(np.float64) - 127.0), 8, axis=1)[..., None]
    return vals.transpose(0, 1, 3, 2).reshape(g * 512, n)


def gelu(v):
    return 0.5 * v * (1.0 + np.tanh(np.sqrt(2.0 / np.pi) * (v + 0.044715 * v**3)))


K, H, N, T, T2, S = 1024, 1024, 512, 2048, 2048, 1024

def setup_inputs():
    n = np.random.standard_normal
    s = mx_kscale(K)[:, None]
    u = mx_kscale(H)[:, None]
    tab_words, tab_scales = pack_weight(n((K, T)) * s, "e4m3")
    w1_words, w1_scales = pack_weight(n((K, H)) / np.sqrt(K) / s * u.T, "e2m1")
    xT = (np.round(16 * n((K, T2))) / 16 * s).astype(np.float32)
    pair = np.random.permutation(T2)
    w2 = (0.7 * n((K, H)) / np.sqrt(K) / s).astype(np.float32)
    b = (0.5 * n(H) * u[:, 0]).astype(np.float32)
    w3_words, w3_scales = pack_weight(n((H, N)) / np.sqrt(H) / u, "e4m3")
    return {"tab_words": tab_words, "tab_scales": tab_scales,
            "offs": striped(np.random.permutation(T)[:S]),
            "xT": xT, "offs2": striped(pair[:S]), "offs3": striped(pair[S:2 * S]),
            "w1_words": w1_words, "w1_scales": w1_scales, "w2": w2, "b": b,
            "w3_words": w3_words, "w3_scales": w3_scales}

def reference(tab_words, tab_scales, offs, xT, offs2, offs3,
              w1_words, w1_scales, w2, b, w3_words, w3_scales):
    v = unpack_weight(tab_words, tab_scales, "e4m3")[:, unstriped(offs)]
    w1 = unpack_weight(w1_words, w1_scales, "e2m1")
    w3 = unpack_weight(w3_words, w3_scales, "e4m3")
    x = f64(xT)[:, unstriped(offs2)] - f64(xT)[:, unstriped(offs3)]
    d = w1.T @ v
    e = mxq(f64(w2), 0, "e4m3").T @ mxq(x, 0, "e4m3")
    h = d / (1.0 + e * e) + f64(b)[:, None]
    return w3.T @ mxq(h, 0, "e4m3")

@@ -1,0 +1,312 @@
+from contextlib import ExitStack
+
+import concourse.mybir as mybir
+from concourse.masks import make_identity
+
+K, H, N, T, S = 1024, 1024, 512, 2048, 1024
+FLOPS = 2 * S * (K * H + K * H + H * N)
+
+F32 = mybir.dt.float32
+BF16 = mybir.dt.bfloat16
+I32 = mybir.dt.int32
+U32 = mybir.dt.uint32
+U16 = mybir.dt.uint16
+U8 = mybir.dt.uint8
+FP8X4 = mybir.dt.float8_e4m3fn_x4
+FP4X4 = mybir.dt.float4_e2m1fn_x4
+ACT = mybir.ActivationFunctionType
+ALU = mybir.AluOpType
+
+P = 128
+CW = 256
+TILES = S // P
+
+
+def tile_list_differential_star_photometry_kernel(
+    tc, tab_words, tab_scales, offs, xT, offs2, offs3, w1_words, w1_scales, w2, b, w3_words, w3_scales, out
+):
+    nc = tc.nc
+    with ExitStack() as ctx:
+        lists = ctx.enter_context(tc.tile_pool(name="lists", bufs=1))
+        sb = ctx.enter_context(tc.tile_pool(name="sb", bufs=1))
+        ps = ctx.enter_context(tc.psum_pool(name="ps", bufs=1))
+
+        def sbuf(shape, dtype, tag):
+            return sb.tile(shape, dtype, name=tag, tag=tag, align_bytes=64)
+
+        def bank(tag):
+            return ps.tile([P, 512], F32, name=tag, tag=tag)
+
+        idx1 = lists.tile([P, S // 16], U16, name="idx1")
+        idx2 = lists.tile([P, S // 16], U16, name="idx2")
+        idx3 = lists.tile([P, S // 16], U16, name="idx3")
+        tab_s = sbuf([P, T], U8, "tab_s")
+        nc.sync.dma_start(idx1[:], offs)
+        nc.sync.dma_start(tab_s[0:32, :].bitcast(I32), tab_scales.rearrange("a q n -> (a q) n").bitcast(I32))
+        nc.sync.dma_start(idx3[:], offs3)
+        nc.sync.dma_start(idx2[:], offs2)
+        nc.vector.memset(tab_s[32:64, :].bitcast(I32), 0)
+        nc.vector.memset(tab_s[64:128, :].bitcast(I32), 0)
+
+        warm = sbuf([P, 2], F32, "warm")
+        nc.vector.memset(warm[:, 0:1], 1.0)
+        nc.scalar.activation(warm[:, 1:2], warm[:, 0:1], ACT.Abs_reciprocal_sqrt)
+
+        planes = {}
+        w2_raw = {}
+
+        def load_plane(a, t):
+            planes[a, t] = sbuf([P, T], F32, "plane%d%d" % (a, t))
+            nc.sync.dma_start(planes[a, t][:], xT[512 * a + t : 512 * (a + 1) : 4, :])
+
+        def load_w2(half, a):
+            w2_raw[half, a] = sbuf([P, 4, 512], F32, "w2raw%d%d" % (half, a))
+            nc.sync.dma_start(
+                w2_raw[half, a][:],
+                w2[512 * a : 512 * (a + 1), 512 * half : 512 * (half + 1)].rearrange("(p t) c -> p t c", t=4),
+            )
+
+        load_plane(0, 0)
+        load_plane(0, 1)
+        load_w2(0, 0)
+        load_plane(0, 2)
+        load_plane(0, 3)
+        load_plane(1, 0)
+        load_w2(0, 1)
+        load_plane(1, 1)
+        load_plane(1, 2)
+        load_plane(1, 3)
+        load_w2(1, 0)
+        load_w2(1, 1)
+        w1_w = sbuf([P, 2, 2 * H], U8, "w1_w")
+        nc.sync.dma_start(w1_w[:].bitcast(I32), w1_words.rearrange("a p n -> p a n").bitcast(I32))
+        tab_w = []
+        for a in range(2):
+            tab_w.append(sbuf([P, T], U32, "tab_w%d" % a))
+            nc.sync.dma_start(tab_w[a][:].bitcast(I32), tab_words[a].rearrange("p n i -> p (n i)").bitcast(I32))
+        w3_w = sbuf([P, 2, N], U32, "w3_w")
+        nc.sync.dma_start(w3_w[:].bitcast(I32), w3_words.rearrange("a p n i -> p a (n i)").bitcast(I32))
+
+        ident = sbuf([P, P], F32, "ident")
+        make_identity(nc, ident[:])
+        b_col = sbuf([P, 2, 4], F32, "b_col")
+        nc.gpsimd.dma_start(b_col[:], b.rearrange("(a p t) -> p a t", a=2, t=4))
+        w1_s = sbuf([P, 2, H], U8, "w1_s")
+        w3_s = sbuf([P, 2, N], U8, "w3_s")
+        v_s = sbuf([P, 2, S], U8, "v_s")
+        nc.gpsimd.memset(w1_s[:].bitcast(I32), 0)
+        nc.gpsimd.memset(v_s[:].bitcast(I32), 0)
+        nc.gpsimd.memset(w3_s[:].bitcast(I32), 0)
+
+        v_rows = sbuf([P, S], U8, "v_rows")
+        nc.vector.tensor_copy(v_rows[:], tab_s[:].indirect(idx1[:]))
+        for q in range(4):
+            nc.gpsimd.dma_start(
+                w1_s[32 * q : 32 * q + 4].bitcast(I32),
+                w1_scales[:, 4 * q : 4 * q + 4, :].rearrange("a r n -> r a n").bitcast(I32),
+            )
+        for a in range(2):
+            for q in range(4):
+                nc.gpsimd.dma_start(
+                    v_s[32 * q : 32 * q + 4, a, :].bitcast(I32),
+                    v_rows[16 * a + 4 * q : 16 * a + 4 * q + 4, :].bitcast(I32),
+                )
+        for q in range(4):
+            nc.gpsimd.dma_start(
+                w3_s[32 * q : 32 * q + 4].bitcast(I32),
+                w3_scales[:, 4 * q : 4 * q + 4, :].rearrange("a r n -> r a n").bitcast(I32),
+            )
+
+        b_rows = sbuf([P, 2, 512], F32, "b_rows")
+        for a in range(2):
+            spread = bank("turn%d" % a)
+            for t in range(4):
+                nc.tensor.transpose(
+                    spread[:, P * t : P * (t + 1)], b_col[:, a, t : t + 1].to_broadcast([P, P]), ident[:]
+                )
+            nc.scalar.copy(b_rows[:, a, :], spread[:])
+
+        def interleave(dst, src):
+            nc.scalar.copy(
+                dst.rearrange("p (c i) t -> p c t i", i=4), src.rearrange("p t (c i) -> p c t i", i=4)
+            )
+
+        def quantize(src, width, tag):
+            codes = sbuf([P, width], U32, tag + "_c")
+            scales = sbuf([P, width], U8, tag + "_s")
+            nc.vector.quantize_mx(out=codes[:].bitcast(FP8X4), scales=scales[:], in_=src)
+            return codes, scales
+
+        w2_q = {}
+
+        def prepare_w2(half, a):
+            rounded = sbuf([P, 512, 4], BF16, "w2b%d" % a)
+            interleave(rounded[:], w2_raw[half, a][:])
+            w2_q[half, a] = quantize(rounded[:].rearrange("p c t -> p (c t)"), 512, "w2q%d%d" % (half, a))
+
+        diff = {}
+        x_q = {}
+        v_w = {}
+
+        def gather_pair(units, tag):
+            comparison = sbuf([P, 2, CW], F32, tag)
+            for u, (c, a, t) in enumerate(units):
+                nc.vector.tensor_copy(comparison[:, u, :], planes[a, t][:].indirect(idx3[:, 16 * c : 16 * (c + 1)]))
+            for u, (c, a, t) in enumerate(units):
+                if t == 0:
+                    diff[c, a] = sbuf([P, 4, CW], F32, "diff%d%d" % (c % 2, a))
+                nc.vector.tensor_tensor(
+                    diff[c, a][:, t, :], planes[a, t][:].indirect(idx2[:, 16 * c : 16 * (c + 1)]),
+                    comparison[:, u, :], ALU.subtract,
+                )
+
+        def prepare_x(c, a, tag):
+            rounded = sbuf([P, CW, 4], BF16, tag)
+            interleave(rounded[:], diff[c, a][:])
+            x_q[c, a] = quantize(rounded[:].rearrange("p c t -> p (c t)"), CW, "xq%d%d" % (c, a))
+
+        def gather_table(c, tag):
+            words = sbuf([P, 2, CW], U32, tag)
+            for a in range(2):
+                v_w[c, a] = words[:, a, :]
+                nc.vector.tensor_copy(v_w[c, a], tab_w[a][:].indirect(idx1[:, 16 * c : 16 * (c + 1)]))
+
+        def place(jt):
+            return jt // 2, slice((jt % 2) * P, (jt % 2 + 1) * P)
+
+        damp = {}
+
+        def damping(jt):
+            c, cols = place(jt)
+            square = sbuf([P, 2, 512], F32, "sq%d" % (jt % 2))
+            for half in range(2):
+                e = bank("e%d" % half)
+                for a in range(2):
+                    nc.tensor.matmul_mx(
+                        e[:],
+                        lhsT=x_q[c, a][0][:, cols].bitcast(FP8X4),
+                        lhsT_scale=x_q[c, a][1][:, cols],
+                        rhs=w2_q[half, a][0][:].bitcast(FP8X4),
+                        rhs_scale=w2_q[half, a][1][:],
+                        start=(a == 0),
+                        stop=(a == 1),
+                    )
+                nc.scalar.activation(
+                    square[:, half, :].rearrange("j (t p) -> j t p", t=4),
+                    e[:].rearrange("j (p t) -> j t p", t=4),
+                    ACT.Square,
+                )
+            root = sbuf([P, 2, 512], F32, "root%d" % (jt % 2))
+            nc.scalar.activation(root[:], square[:], ACT.Abs_reciprocal_sqrt, bias=1.0)
+            damp[jt] = sbuf([P, 2, 512], F32, "w2raw%d%d" % (jt % 4 // 2, jt % 2))
+            nc.scalar.activation(damp[jt][:], root[:], ACT.Square)
+
+        h_q = {}
+
+        def hidden(jt, eng):
+            c, cols = place(jt)
+            rounded = sbuf([P, 2, P, 4], BF16, "hb%d" % jt)
+            for half in range(2):
+                d = bank("d%d" % half)
+                for a in range(2):
+                    nc.tensor.matmul_mx(
+                        d[:],
+                        lhsT=v_w[c, a][:, cols].bitcast(FP8X4),
+                        lhsT_scale=v_s[:, a, jt * P : (jt + 1) * P],
+                        rhs=w1_w[:, a, 1024 * half : 1024 * (half + 1)].bitcast(FP4X4),
+                        rhs_scale=w1_s[:, a, 512 * half : 512 * (half + 1)],
+                        start=(a == 0),
+                        stop=(a == 1),
+                    )
+                damped = sbuf([P, 512], F32, "m%d%d" % (jt % 2, half))
+                nc.vector.tensor_tensor(
+                    damped[:].rearrange("j (t p) -> j t p", t=4),
+                    d[:].rearrange("j (p t) -> j t p", t=4),
+                    damp[jt][:, half, :].rearrange("j (t p) -> j t p", t=4),
+                    ALU.mult,
+                )
+                turned = bank("turn%d" % half)
+                for t in range(4):
+                    nc.tensor.matmul(
+                        turned[:, P * t : P * (t + 1)], b_rows[:, half, P * t : P * (t + 1)], ident[:],
+                        start=(t == 0), stop=False, is_transpose=True,
+                    )
+                for t in range(4):
+                    nc.tensor.matmul(
+                        turned[:, P * t : P * (t + 1)], damped[:, P * t : P * (t + 1)], ident[:],
+                        start=False, stop=(t == 3), is_transpose=True,
+                    )
+                eng[half](rounded[:, half], turned[:].rearrange("p (t j) -> p j t", t=4))
+            h_q[jt] = quantize(rounded[:].rearrange("p a j t -> p (a j t)"), 2 * P, "hq%d" % (jt % 2))
+
+        def scores(jt, eng):
+            acc = bank("o%d" % (jt % 2))
+            for nt in range(4):
+                for a in range(2):
+                    nc.tensor.matmul_mx(
+                        acc[:, P * nt : P * (nt + 1)],
+                        lhsT=w3_w[:, a, P * nt : P * (nt + 1)].bitcast(FP8X4),
+                        lhsT_scale=w3_s[:, a, P * nt : P * (nt + 1)],
+                        rhs=h_q[jt][0][:, P * a : P * (a + 1)].bitcast(FP8X4),
+                        rhs_scale=h_q[jt][1][:, P * a : P * (a + 1)],
+                        start=(a == 0),
+                        stop=(a == 1),
+                    )
+            result = sbuf([P, 4, P], F32, "res%d" % (jt % 2))
+            eng(result[:].rearrange("p n j -> p (n j)"), acc[:])
+            nc.sync.dma_start(out[:, jt * P : (jt + 1) * P].rearrange("(n p) j -> p n j", p=P), result[:])
+
+        A = nc.scalar.copy
+        V = nc.vector.tensor_copy
+        for t in range(4):
+            gather_pair([(0, 0, t), (1, 0, t)], "cmp%d" % (t % 2))
+        prepare_w2(0, 0)
+        prepare_x(0, 0, "xb0")
+        prepare_x(1, 0, "xb1")
+        prepare_w2(0, 1)
+        for t in range(4):
+            gather_pair([(0, 1, t), (1, 1, t)], "cmp%d" % (t % 2))
+        prepare_w2(1, 0)
+        prepare_w2(1, 1)
+        prepare_x(0, 1, "w2raw10")
+        prepare_x(1, 1, "w2raw11")
+        damping(0)
+        gather_pair([(2, 0, 0), (2, 0, 1)], "w2raw10")
+        gather_table(0, "w2b1")
+        damping(1)
+        gather_pair([(2, 0, 2), (2, 0, 3)], "w2raw11")
+        hidden(0, (A, A))
+        damping(2)
+        gather_pair([(2, 1, 0), (2, 1, 1)], "w2raw00")
+        prepare_x(2, 0, "root0")
+        hidden(1, (A, A))
+        gather_table(1, "hb0")
+        scores(0, A)
+        gather_pair([(2, 1, 2), (2, 1, 3)], "w2raw01")
+        damping(3)
+        hidden(2, (A, A))
+        prepare_x(2, 1, "sq0")
+        gather_pair([(3, 0, 0), (3, 0, 1)], "hb1")
+        scores(1, A)
+        gather_pair([(3, 0, 2), (3, 0, 3)], "w2raw10")
+        damping(4)
+        hidden(3, (A, A))
+        gather_table(2, "hb2")
+        gather_pair([(3, 1, 0), (3, 1, 1)], "w2raw11")
+        prepare_x(3, 0, "root1")
+        scores(2, A)
+        gather_pair([(3, 1, 2), (3, 1, 3)], "sq0")
+        damping(5)
+        hidden(4, (A, A))
+        prepare_x(3, 1, "root0")
+        gather_table(3, "w2raw00")
+        scores(3, A)
+        damping(6)
+        hidden(5, (A, A))
+        scores(4, A)
+        damping(7)
+        hidden(6, (V, V))
+        scores(5, A)
+        hidden(7, (A, V))
+        scores(6, A)
+        scores(7, A)

@@ -45,12 +45,18 @@ def tile_list_differential_star_photometry_kernel(
         nc.sync.dma_start(tab_s[0:32, :].bitcast(I32), tab_scales.rearrange("a q n -> (a q) n").bitcast(I32))
         nc.sync.dma_start(idx3[:], offs3)
         nc.sync.dma_start(idx2[:], offs2)
+        w1_s = sbuf([P, 2, H], U8, "w1_s")
+        v_s = sbuf([P, 2, S], U8, "v_s")
+        w3_s = sbuf([P, 2, N], U8, "w3_s")
         nc.vector.memset(tab_s[32:64, :].bitcast(I32), 0)
         nc.vector.memset(tab_s[64:128, :].bitcast(I32), 0)
-
-        warm = sbuf([P, 2], F32, "warm")
-        nc.vector.memset(warm[:, 0:1], 1.0)
-        nc.scalar.activation(warm[:, 1:2], warm[:, 0:1], ACT.Abs_reciprocal_sqrt)
+        ident = sbuf([P, P], F32, "ident")
+        make_identity(nc, ident[:])
+        nc.gpsimd.memset(w1_s[:].bitcast(I32), 0)
+        nc.gpsimd.memset(v_s[:].bitcast(I32), 0)
+        nc.gpsimd.memset(w3_s[:].bitcast(I32), 0)
+        v_rows = sbuf([P, S], U8, "v_rows")
+        nc.vector.tensor_copy(v_rows[:], tab_s[:].indirect(idx1[:]))
 
         planes = {}
         w2_raw = {}
@@ -69,67 +75,66 @@ def tile_list_differential_star_photometry_kernel(
         load_plane(0, 0)
         load_plane(0, 1)
         load_w2(0, 0)
+        b_col = sbuf([P, 2, 4], F32, "b_col")
+        nc.sync.dma_start(b_col[:], b.rearrange("(a p t) -> p a t", a=2, t=4))
         load_plane(0, 2)
         load_plane(0, 3)
-        load_plane(1, 0)
         load_w2(0, 1)
+        load_plane(1, 0)
+        load_w2(1, 0)
+        load_w2(1, 1)
         load_plane(1, 1)
         load_plane(1, 2)
         load_plane(1, 3)
-        load_w2(1, 0)
-        load_w2(1, 1)
-        w1_w = sbuf([P, 2, 2 * H], U8, "w1_w")
-        nc.sync.dma_start(w1_w[:].bitcast(I32), w1_words.rearrange("a p n -> p a n").bitcast(I32))
         tab_w = []
-        for a in range(2):
+
+        def load_table(a):
             tab_w.append(sbuf([P, T], U32, "tab_w%d" % a))
             nc.sync.dma_start(tab_w[a][:].bitcast(I32), tab_words[a].rearrange("p n i -> p (n i)").bitcast(I32))
-        w3_w = sbuf([P, 2, N], U32, "w3_w")
-        nc.sync.dma_start(w3_w[:].bitcast(I32), w3_words.rearrange("a p n i -> p a (n i)").bitcast(I32))
 
-        ident = sbuf([P, P], F32, "ident")
-        make_identity(nc, ident[:])
-        b_col = sbuf([P, 2, 4], F32, "b_col")
-        nc.gpsimd.dma_start(b_col[:], b.rearrange("(a p t) -> p a t", a=2, t=4))
-        w1_s = sbuf([P, 2, H], U8, "w1_s")
-        w3_s = sbuf([P, 2, N], U8, "w3_s")
-        v_s = sbuf([P, 2, S], U8, "v_s")
-        nc.gpsimd.memset(w1_s[:].bitcast(I32), 0)
-        nc.gpsimd.memset(v_s[:].bitcast(I32), 0)
-        nc.gpsimd.memset(w3_s[:].bitcast(I32), 0)
-
-        v_rows = sbuf([P, S], U8, "v_rows")
-        nc.vector.tensor_copy(v_rows[:], tab_s[:].indirect(idx1[:]))
-        for q in range(4):
-            nc.gpsimd.dma_start(
-                w1_s[32 * q : 32 * q + 4].bitcast(I32),
-                w1_scales[:, 4 * q : 4 * q + 4, :].rearrange("a r n -> r a n").bitcast(I32),
-            )
-        for a in range(2):
+        def load_scales(plane, rows):
             for q in range(4):
-                nc.gpsimd.dma_start(
+                nc.sync.dma_start(
+                    plane[32 * q : 32 * q + 4].bitcast(I32),
+                    rows[:, 4 * q : 4 * q + 4, :].rearrange("a r n -> r a n").bitcast(I32),
+                )
+
+        def move_scales(a):
+            for q in range(4):
+                nc.sync.dma_start(
                     v_s[32 * q : 32 * q + 4, a, :].bitcast(I32),
                     v_rows[16 * a + 4 * q : 16 * a + 4 * q + 4, :].bitcast(I32),
                 )
-        for q in range(4):
-            nc.gpsimd.dma_start(
-                w3_s[32 * q : 32 * q + 4].bitcast(I32),
-                w3_scales[:, 4 * q : 4 * q + 4, :].rearrange("a r n -> r a n").bitcast(I32),
-            )
+
+        load_table(0)
+        load_scales(w1_s, w1_scales)
+        load_table(1)
+        move_scales(0)
+        w1_w = sbuf([P, 2, 2 * H], U8, "w1_w")
+        nc.sync.dma_start(w1_w[:].bitcast(I32), w1_words.rearrange("a p n -> p a n").bitcast(I32))
+        move_scales(1)
+        w3_w = sbuf([P, 2, N], U32, "w3_w")
+        nc.sync.dma_start(w3_w[:].bitcast(I32), w3_words.rearrange("a p n i -> p a (n i)").bitcast(I32))
+        load_scales(w3_s, w3_scales)
+
 
         b_rows = sbuf([P, 2, 512], F32, "b_rows")
         for a in range(2):
-            spread = bank("turn%d" % a)
+            spread = bank("turn%d" % (a % 2))
             for t in range(4):
                 nc.tensor.transpose(
                     spread[:, P * t : P * (t + 1)], b_col[:, a, t : t + 1].to_broadcast([P, P]), ident[:]
                 )
             nc.scalar.copy(b_rows[:, a, :], spread[:])
+        b_rep = sbuf([P, 2, P, 4], F32, "b_rep")
+        for a in range(2):
+            nc.scalar.copy(b_rep[:, a], b_col[:, a : a + 1, :].to_broadcast([P, P, 4]))
 
-        def interleave(dst, src):
-            nc.scalar.copy(
-                dst.rearrange("p (c i) t -> p c t i", i=4), src.rearrange("p t (c i) -> p c t i", i=4)
-            )
+        A = nc.scalar.copy
+        V = nc.vector.tensor_copy
+
+        def interleave(eng, dst, src):
+            eng(dst.rearrange("p (c i) t -> p c t i", i=4), src.rearrange("p t (c i) -> p c t i", i=4))
 
         def quantize(src, width, tag):
             codes = sbuf([P, width], U32, tag + "_c")
@@ -141,51 +146,54 @@ def tile_list_differential_star_photometry_kernel(
 
         def prepare_w2(half, a):
             rounded = sbuf([P, 512, 4], BF16, "w2b%d" % a)
-            interleave(rounded[:], w2_raw[half, a][:])
+            interleave(A, rounded[:], w2_raw[half, a][:])
             w2_q[half, a] = quantize(rounded[:].rearrange("p c t -> p (c t)"), 512, "w2q%d%d" % (half, a))
 
         diff = {}
         x_q = {}
         v_w = {}
 
-        def gather_pair(units, tag):
-            comparison = sbuf([P, 2, CW], F32, tag)
-            for u, (c, a, t) in enumerate(units):
-                nc.vector.tensor_copy(comparison[:, u, :], planes[a, t][:].indirect(idx3[:, 16 * c : 16 * (c + 1)]))
-            for u, (c, a, t) in enumerate(units):
-                if t == 0:
-                    diff[c, a] = sbuf([P, 4, CW], F32, "diff%d%d" % (c % 2, a))
+        def gather(units, tag):
+            comparison = sbuf([P, sum(u[1] for u in units)], F32, tag)
+            at = [sum(u[1] for u in units[:i]) for i in range(len(units))]
+            for c0, (lo, n, a, t) in zip(at, units):
+                nc.vector.tensor_copy(
+                    comparison[:, c0 : c0 + n], planes[a, t][:].indirect(idx3[:, lo // 16 : (lo + n) // 16])
+                )
+            for c0, (lo, n, a, t) in zip(at, units):
                 nc.vector.tensor_tensor(
-                    diff[c, a][:, t, :], planes[a, t][:].indirect(idx2[:, 16 * c : 16 * (c + 1)]),
-                    comparison[:, u, :], ALU.subtract,
+                    diff[lo, a][:, t, :], planes[a, t][:].indirect(idx2[:, lo // 16 : (lo + n) // 16]),
+                    comparison[:, c0 : c0 + n], ALU.subtract,
                 )
 
-        def prepare_x(c, a, tag):
-            rounded = sbuf([P, CW, 4], BF16, tag)
-            interleave(rounded[:], diff[c, a][:])
-            x_q[c, a] = quantize(rounded[:].rearrange("p c t -> p (c t)"), CW, "xq%d%d" % (c, a))
+        def new_diff(lo, n, a, tag):
+            diff[lo, a] = sbuf([P, 4, n], F32, tag)
+
+        def prepare_x(eng, lo, n, a, tag):
+            rounded = sbuf([P, n, 4], BF16, tag)
+            interleave(eng, rounded[:], diff[lo, a][:])
+            codes, scales = quantize(rounded[:].rearrange("p c t -> p (c t)"), n, "xq%d_%d" % (lo, a))
+            for i in range(n // P):
+                x_q[lo // P + i, a] = (codes[:, P * i : P * (i + 1)], scales[:, P * i : P * (i + 1)])
 
         def gather_table(c, tag):
             words = sbuf([P, 2, CW], U32, tag)
             for a in range(2):
-                v_w[c, a] = words[:, a, :]
-                nc.vector.tensor_copy(v_w[c, a], tab_w[a][:].indirect(idx1[:, 16 * c : 16 * (c + 1)]))
-
-        def place(jt):
-            return jt // 2, slice((jt % 2) * P, (jt % 2 + 1) * P)
+                nc.vector.tensor_copy(words[:, a, :], tab_w[a][:].indirect(idx1[:, 16 * c : 16 * (c + 1)]))
+                for i in range(2):
+                    v_w[2 * c + i, a] = words[:, a, P * i : P * (i + 1)]
 
         damp = {}
 
-        def damping(jt):
-            c, cols = place(jt)
+        def damping(jt, tag, split=False):
             square = sbuf([P, 2, 512], F32, "sq%d" % (jt % 2))
             for half in range(2):
-                e = bank("e%d" % half)
+                e = bank("e%d" % ((2 * jt + half) % 2))
                 for a in range(2):
                     nc.tensor.matmul_mx(
                         e[:],
-                        lhsT=x_q[c, a][0][:, cols].bitcast(FP8X4),
-                        lhsT_scale=x_q[c, a][1][:, cols],
+                        lhsT=x_q[jt, a][0].bitcast(FP8X4),
+                        lhsT_scale=x_q[jt, a][1],
                         rhs=w2_q[half, a][0][:].bitcast(FP8X4),
                         rhs_scale=w2_q[half, a][1][:],
                         start=(a == 0),
@@ -197,50 +205,63 @@ def tile_list_differential_star_photometry_kernel(
                     ACT.Square,
                 )
             root = sbuf([P, 2, 512], F32, "root%d" % (jt % 2))
-            nc.scalar.activation(root[:], square[:], ACT.Abs_reciprocal_sqrt, bias=1.0)
-            damp[jt] = sbuf([P, 2, 512], F32, "w2raw%d%d" % (jt % 4 // 2, jt % 2))
-            nc.scalar.activation(damp[jt][:], root[:], ACT.Square)
+            damp[jt] = sbuf([P, 2, 512], F32, tag)
+            parts = [slice(0, 1), slice(1, 2)] if split else [slice(0, 2)]
+            for part in parts:
+                nc.scalar.activation(root[:, part], square[:, part], ACT.Abs_reciprocal_sqrt, bias=1.0)
+            for part in parts:
+                nc.scalar.activation(damp[jt][:, part], root[:, part], ACT.Square)
 
-        h_q = {}
+        damped = {}
 
-        def hidden(jt, eng):
-            c, cols = place(jt)
-            rounded = sbuf([P, 2, P, 4], BF16, "hb%d" % jt)
+        def product(jt):
             for half in range(2):
-                d = bank("d%d" % half)
+                d = bank("d%d" % ((2 * jt + half) % 3))
                 for a in range(2):
                     nc.tensor.matmul_mx(
                         d[:],
-                        lhsT=v_w[c, a][:, cols].bitcast(FP8X4),
+                        lhsT=v_w[jt, a].bitcast(FP8X4),
                         lhsT_scale=v_s[:, a, jt * P : (jt + 1) * P],
                         rhs=w1_w[:, a, 1024 * half : 1024 * (half + 1)].bitcast(FP4X4),
                         rhs_scale=w1_s[:, a, 512 * half : 512 * (half + 1)],
                         start=(a == 0),
                         stop=(a == 1),
                     )
-                damped = sbuf([P, 512], F32, "m%d%d" % (jt % 2, half))
+                damped[jt, half] = sbuf([P, 512], F32, "m%d%d" % (jt % 2, half))
                 nc.vector.tensor_tensor(
-                    damped[:].rearrange("j (t p) -> j t p", t=4),
+                    damped[jt, half][:].rearrange("j (t p) -> j t p", t=4),
                     d[:].rearrange("j (p t) -> j t p", t=4),
                     damp[jt][:, half, :].rearrange("j (t p) -> j t p", t=4),
                     ALU.mult,
                 )
-                turned = bank("turn%d" % half)
+
+        h_q = {}
+
+        def hidden(jt, engines, tag):
+            rounded = sbuf([P, 2, P, 4], BF16, tag)
+            for half in range(2):
+                turned = bank("turn%d" % ((2 * jt + half) % 2))
+                on_scalar = engines[half] == "A"
+                if on_scalar:
+                    for t in range(4):
+                        nc.tensor.matmul(
+                            turned[:, P * t : P * (t + 1)], b_rows[:, half, P * t : P * (t + 1)], ident[:],
+                            start=(t == 0), stop=False, is_transpose=True,
+                        )
                 for t in range(4):
                     nc.tensor.matmul(
-                        turned[:, P * t : P * (t + 1)], b_rows[:, half, P * t : P * (t + 1)], ident[:],
-                        start=(t == 0), stop=False, is_transpose=True,
+                        turned[:, P * t : P * (t + 1)], damped[jt, half][:, P * t : P * (t + 1)], ident[:],
+                        start=(t == 0 and not on_scalar), stop=(t == 3), is_transpose=True,
                     )
-                for t in range(4):
-                    nc.tensor.matmul(
-                        turned[:, P * t : P * (t + 1)], damped[:, P * t : P * (t + 1)], ident[:],
-                        start=False, stop=(t == 3), is_transpose=True,
-                    )
-                eng[half](rounded[:, half], turned[:].rearrange("p (t j) -> p j t", t=4))
+                view = turned[:].rearrange("p (t j) -> p j t", t=4)
+                if on_scalar:
+                    nc.scalar.copy(rounded[:, half], view)
+                else:
+                    nc.vector.tensor_tensor(rounded[:, half], view, b_rep[:, half], ALU.add)
             h_q[jt] = quantize(rounded[:].rearrange("p a j t -> p (a j t)"), 2 * P, "hq%d" % (jt % 2))
 
         def scores(jt, eng):
-            acc = bank("o%d" % (jt % 2))
+            acc = bank("o%d" % (jt % 1))
             for nt in range(4):
                 for a in range(2):
                     nc.tensor.matmul_mx(
@@ -256,57 +277,67 @@ def tile_list_differential_star_photometry_kernel(
             eng(result[:].rearrange("p n j -> p (n j)"), acc[:])
             nc.sync.dma_start(out[:, jt * P : (jt + 1) * P].rearrange("(n p) j -> p n j", p=P), result[:])
 
-        A = nc.scalar.copy
-        V = nc.vector.tensor_copy
+        new_diff(0, 512, 0, "diffA")
+        new_diff(512, 256, 0, "diffB")
+        new_diff(0, 256, 1, "diffC")
+        new_diff(256, 256, 1, "diffD")
+        new_diff(512, 256, 1, "diffE")
         for t in range(4):
-            gather_pair([(0, 0, t), (1, 0, t)], "cmp%d" % (t % 2))
-        prepare_w2(0, 0)
-        prepare_x(0, 0, "xb0")
-        prepare_x(1, 0, "xb1")
-        prepare_w2(0, 1)
-        for t in range(4):
-            gather_pair([(0, 1, t), (1, 1, t)], "cmp%d" % (t % 2))
+            gather([(0, 512, 0, t), (512, 256, 0, t)], "cmp%d" % (t % 2))
+            if t % 2:
+                prepare_w2(0, t // 2)
+        prepare_x(A, 0, 512, 0, "w2raw01")
+        prepare_x(A, 512, 256, 0, "diffA")
+        gather([(0, 256, 1, 0), (256, 256, 1, 0), (512, 256, 1, 0)], "cmp0")
         prepare_w2(1, 0)
         prepare_w2(1, 1)
-        prepare_x(0, 1, "w2raw10")
-        prepare_x(1, 1, "w2raw11")
-        damping(0)
-        gather_pair([(2, 0, 0), (2, 0, 1)], "w2raw10")
+        for t in range(1, 4):
+            gather([(0, 256, 1, t), (256, 256, 1, t)], "cmp%d" % (t % 2))
+        prepare_x(A, 0, 256, 1, "xb0")
+        prepare_x(A, 256, 256, 1, "xb1")
+        gather([(512, 256, 1, 1), (512, 256, 1, 2)], "xb0")
+        new_diff(768, 256, 0, "diffB")
+        gather([(512, 256, 1, 3), (768, 256, 0, 0)], "xb1")
         gather_table(0, "w2b1")
-        damping(1)
-        gather_pair([(2, 0, 2), (2, 0, 3)], "w2raw11")
-        hidden(0, (A, A))
-        damping(2)
-        gather_pair([(2, 1, 0), (2, 1, 1)], "w2raw00")
-        prepare_x(2, 0, "root0")
-        hidden(1, (A, A))
-        gather_table(1, "hb0")
+        damping(0, "w2raw00")
+        damping(1, "w2raw01")
+        product(0)
+        gather([(768, 256, 0, 1), (768, 256, 0, 2)], "w2raw00")
+        prepare_x(A, 512, 256, 1, "xbB")
+        new_diff(768, 256, 1, "diffC")
+        gather([(768, 256, 0, 3), (768, 256, 1, 0)], "xbB")
+        damping(2, "w2raw10")
+        product(1)
+        gather_table(1, "w2raw01")
+        hidden(0, "AA", "hb0")
+        gather([(768, 256, 1, 1), (768, 256, 1, 2), (768, 256, 1, 3)], "hb0")
+        damping(3, "w2raw11")
+        product(2)
+        prepare_x(A, 768, 256, 0, "xb0")
+        hidden(1, "AA", "hb1")
+        prepare_x(V, 768, 256, 1, "xb1")
+        damping(4, "w2raw00")
+        product(3)
+        gather_table(2, "w2raw11")
         scores(0, A)
-        gather_pair([(2, 1, 2), (2, 1, 3)], "w2raw01")
-        damping(3)
-        hidden(2, (A, A))
-        prepare_x(2, 1, "sq0")
-        gather_pair([(3, 0, 0), (3, 0, 1)], "hb1")
-        scores(1, A)
-        gather_pair([(3, 0, 2), (3, 0, 3)], "w2raw10")
-        damping(4)
-        hidden(3, (A, A))
-        gather_table(2, "hb2")
-        gather_pair([(3, 1, 0), (3, 1, 1)], "w2raw11")
-        prepare_x(3, 0, "root1")
-        scores(2, A)
-        gather_pair([(3, 1, 2), (3, 1, 3)], "sq0")
-        damping(5)
-        hidden(4, (A, A))
-        prepare_x(3, 1, "root0")
+        hidden(2, "AA", "tab_s")
+        damping(5, "w2raw10")
+        product(4)
         gather_table(3, "w2raw00")
-        scores(3, A)
-        damping(6)
-        hidden(5, (A, A))
+        scores(1, A)
+        hidden(3, "VV", "hb1")
+        damping(6, "w2raw01")
+        product(5)
+        scores(2, V)
+        hidden(4, "VV", "tab_s")
+        damping(7, "w2raw10", True)
+        product(6)
+        scores(3, V)
+        hidden(5, "VV", "hb1")
         scores(4, A)
-        damping(7)
-        hidden(6, (V, V))
+        hidden(6, "AA", "tab_s")
+        product(7)
         scores(5, A)
-        hidden(7, (A, V))
+        hidden(7, "AV", "hb1")
         scores(6, A)
         scores(7, A)

@@ -200,8 +200,8 @@ def tile_list_differential_star_photometry_kernel(
                         stop=(a == 1),
                     )
                 nc.scalar.activation(
-                    square[:, half, :].rearrange("j (t p) -> j t p", t=4),
-                    e[:].rearrange("j (p t) -> j t p", t=4),
+                    square[:, half, :].rearrange("j (t c i) -> j c t i", t=4, i=4),
+                    e[:].rearrange("j (c i t) -> j c t i", t=4, i=4),
                     ACT.Square,
                 )
             root = sbuf([P, 2, 512], F32, "root%d" % (jt % 2))
@@ -229,9 +229,9 @@ def tile_list_differential_star_photometry_kernel(
                     )
                 damped[jt, half] = sbuf([P, 512], F32, "m%d%d" % (jt % 2, half))
                 nc.vector.tensor_tensor(
-                    damped[jt, half][:].rearrange("j (t p) -> j t p", t=4),
-                    d[:].rearrange("j (p t) -> j t p", t=4),
-                    damp[jt][:, half, :].rearrange("j (t p) -> j t p", t=4),
+                    damped[jt, half][:].rearrange("j (t c i) -> j c t i", t=4, i=4),
+                    d[:].rearrange("j (c i t) -> j c t i", t=4, i=4),
+                    damp[jt][:, half, :].rearrange("j (t c i) -> j c t i", t=4, i=4),
                     ALU.mult,
                 )
 

@@ -73,19 +73,17 @@ def tile_list_differential_star_photometry_kernel(
             )
 
         load_plane(0, 0)
-        load_plane(0, 1)
         load_w2(0, 0)
         b_col = sbuf([P, 2, 4], F32, "b_col")
         nc.sync.dma_start(b_col[:], b.rearrange("(a p t) -> p a t", a=2, t=4))
-        load_plane(0, 2)
-        load_plane(0, 3)
+        load_plane(0, 1)
         load_w2(0, 1)
-        load_plane(1, 0)
+        load_plane(0, 2)
         load_w2(1, 0)
+        load_plane(0, 3)
         load_w2(1, 1)
-        load_plane(1, 1)
-        load_plane(1, 2)
-        load_plane(1, 3)
+        for t in range(4):
+            load_plane(1, t)
         tab_w = []
 
         def load_table(a):
@@ -120,12 +118,13 @@ def tile_list_differential_star_photometry_kernel(
 
         b_rows = sbuf([P, 2, 512], F32, "b_rows")
         for a in range(2):
-            spread = bank("turn%d" % (a % 2))
+            spread = bank("turn%d" % a)
             for t in range(4):
                 nc.tensor.transpose(
                     spread[:, P * t : P * (t + 1)], b_col[:, a, t : t + 1].to_broadcast([P, P]), ident[:]
                 )
             nc.scalar.copy(b_rows[:, a, :], spread[:])
+
         b_rep = sbuf([P, 2, P, 4], F32, "b_rep")
         for a in range(2):
             nc.scalar.copy(b_rep[:, a], b_col[:, a : a + 1, :].to_broadcast([P, P, 4]))
@@ -136,8 +135,8 @@ def tile_list_differential_star_photometry_kernel(
         def interleave(eng, dst, src):
             eng(dst.rearrange("p (c i) t -> p c t i", i=4), src.rearrange("p t (c i) -> p c t i", i=4))
 
-        def quantize(src, width, tag):
-            codes = sbuf([P, width], U32, tag + "_c")
+        def quantize(src, width, tag, codes_tag=None):
+            codes = sbuf([P, width], U32, codes_tag or tag + "_c")
             scales = sbuf([P, width], U8, tag + "_s")
             nc.vector.quantize_mx(out=codes[:].bitcast(FP8X4), scales=scales[:], in_=src)
             return codes, scales
@@ -161,34 +160,35 @@ def tile_list_differential_star_photometry_kernel(
                     comparison[:, c0 : c0 + n], planes[a, t][:].indirect(idx3[:, lo // 16 : (lo + n) // 16])
                 )
             for c0, (lo, n, a, t) in zip(at, units):
+                base = max(k for k, pas in diff if pas == a and k <= lo)
                 nc.vector.tensor_tensor(
-                    diff[lo, a][:, t, :], planes[a, t][:].indirect(idx2[:, lo // 16 : (lo + n) // 16]),
+                    diff[base, a][:, t, lo - base : lo - base + n], planes[a, t][:].indirect(idx2[:, lo // 16 : (lo + n) // 16]),
                     comparison[:, c0 : c0 + n], ALU.subtract,
                 )
 
         def new_diff(lo, n, a, tag):
             diff[lo, a] = sbuf([P, 4, n], F32, tag)
 
-        def prepare_x(eng, lo, n, a, tag):
+        def prepare_x(eng, lo, n, a, tag, base, codes_tag=None):
             rounded = sbuf([P, n, 4], BF16, tag)
-            interleave(eng, rounded[:], diff[lo, a][:])
-            codes, scales = quantize(rounded[:].rearrange("p c t -> p (c t)"), n, "xq%d_%d" % (lo, a))
+            interleave(eng, rounded[:], diff[base, a][:, :, lo - base : lo - base + n])
+            codes, scales = quantize(rounded[:].rearrange("p c t -> p (c t)"), n, "xq%d_%d" % (lo, a), codes_tag)
             for i in range(n // P):
                 x_q[lo // P + i, a] = (codes[:, P * i : P * (i + 1)], scales[:, P * i : P * (i + 1)])
 
-        def gather_table(c, tag):
-            words = sbuf([P, 2, CW], U32, tag)
+        def gather_table(lo, n, tag):
+            words = sbuf([P, 2, n], U32, tag)
             for a in range(2):
-                nc.vector.tensor_copy(words[:, a, :], tab_w[a][:].indirect(idx1[:, 16 * c : 16 * (c + 1)]))
-                for i in range(2):
-                    v_w[2 * c + i, a] = words[:, a, P * i : P * (i + 1)]
+                nc.vector.tensor_copy(words[:, a, :], tab_w[a][:].indirect(idx1[:, lo // 16 : (lo + n) // 16]))
+                for i in range(n // P):
+                    v_w[lo // P + i, a] = words[:, a, P * i : P * (i + 1)]
 
         damp = {}
 
-        def damping(jt, tag, split=False):
+        def damping(jt, tag, banks, split=False):
             square = sbuf([P, 2, 512], F32, "sq%d" % (jt % 2))
             for half in range(2):
-                e = bank("e%d" % ((2 * jt + half) % 2))
+                e = bank(banks[half])
                 for a in range(2):
                     nc.tensor.matmul_mx(
                         e[:],
@@ -204,7 +204,7 @@ def tile_list_differential_star_photometry_kernel(
                     e[:].rearrange("j (c i t) -> j c t i", t=4, i=4),
                     ACT.Square,
                 )
-            root = sbuf([P, 2, 512], F32, "root%d" % (jt % 2))
+            root = sbuf([P, 2, 512], F32, "m0" if jt == 2 else "root%d" % (jt % 2))
             damp[jt] = sbuf([P, 2, 512], F32, tag)
             parts = [slice(0, 1), slice(1, 2)] if split else [slice(0, 2)]
             for part in parts:
@@ -214,9 +214,10 @@ def tile_list_differential_star_photometry_kernel(
 
         damped = {}
 
-        def product(jt):
+        def product(jt, tag):
+            both = sbuf([P, 2, 512], F32, tag)
             for half in range(2):
-                d = bank("d%d" % ((2 * jt + half) % 3))
+                d = bank("d%d" % half)
                 for a in range(2):
                     nc.tensor.matmul_mx(
                         d[:],
@@ -227,9 +228,9 @@ def tile_list_differential_star_photometry_kernel(
                         start=(a == 0),
                         stop=(a == 1),
                     )
-                damped[jt, half] = sbuf([P, 512], F32, "m%d%d" % (jt % 2, half))
+                damped[jt, half] = both[:, half, :]
                 nc.vector.tensor_tensor(
-                    damped[jt, half][:].rearrange("j (t c i) -> j c t i", t=4, i=4),
+                    damped[jt, half].rearrange("j (t c i) -> j c t i", t=4, i=4),
                     d[:].rearrange("j (c i t) -> j c t i", t=4, i=4),
                     damp[jt][:, half, :].rearrange("j (t c i) -> j c t i", t=4, i=4),
                     ALU.mult,
@@ -240,7 +241,7 @@ def tile_list_differential_star_photometry_kernel(
         def hidden(jt, engines, tag):
             rounded = sbuf([P, 2, P, 4], BF16, tag)
             for half in range(2):
-                turned = bank("turn%d" % ((2 * jt + half) % 2))
+                turned = bank("turn%d" % half)
                 on_scalar = engines[half] == "A"
                 if on_scalar:
                     for t in range(4):
@@ -260,8 +261,8 @@ def tile_list_differential_star_photometry_kernel(
                     nc.vector.tensor_tensor(rounded[:, half], view, b_rep[:, half], ALU.add)
             h_q[jt] = quantize(rounded[:].rearrange("p a j t -> p (a j t)"), 2 * P, "hq%d" % (jt % 2))
 
-        def scores(jt, eng):
-            acc = bank("o%d" % (jt % 1))
+        def scores(jt, eng, tag):
+            acc = bank("o%d" % (jt % 2))
             for nt in range(4):
                 for a in range(2):
                     nc.tensor.matmul_mx(
@@ -273,71 +274,42 @@ def tile_list_differential_star_photometry_kernel(
                         start=(a == 0),
                         stop=(a == 1),
                     )
-            result = sbuf([P, 4, P], F32, "res%d" % (jt % 2))
+            result = sbuf([P, 4, P], F32, tag)
             eng(result[:].rearrange("p n j -> p (n j)"), acc[:])
             nc.sync.dma_start(out[:, jt * P : (jt + 1) * P].rearrange("(n p) j -> p n j", p=P), result[:])
 
-        new_diff(0, 512, 0, "diffA")
-        new_diff(512, 256, 0, "diffB")
-        new_diff(0, 256, 1, "diffC")
-        new_diff(256, 256, 1, "diffD")
-        new_diff(512, 256, 1, "diffE")
+        new_diff(0, 1024, 0, "diffA")
+        new_diff(0, 512, 1, "diffC")
         for t in range(4):
-            gather([(0, 512, 0, t), (512, 256, 0, t)], "cmp%d" % (t % 2))
-            if t % 2:
-                prepare_w2(0, t // 2)
-        prepare_x(A, 0, 512, 0, "w2raw01")
-        prepare_x(A, 512, 256, 0, "diffA")
-        gather([(0, 256, 1, 0), (256, 256, 1, 0), (512, 256, 1, 0)], "cmp0")
+            gather([(0, 1024, 0, t)], "cmp%d" % (t % 2))
+        prepare_w2(0, 0)
+        prepare_w2(0, 1)
+        prepare_x(A, 0, 512, 0, "w2raw01", 0)
+        for t in range(3):
+            gather([(0, 512, 1, t)], "cmp%d" % (t % 2))
         prepare_w2(1, 0)
+        prepare_x(A, 512, 512, 0, "w2raw10", 0)
         prepare_w2(1, 1)
-        for t in range(1, 4):
-            gather([(0, 256, 1, t), (256, 256, 1, t)], "cmp%d" % (t % 2))
-        prepare_x(A, 0, 256, 1, "xb0")
-        prepare_x(A, 256, 256, 1, "xb1")
-        gather([(512, 256, 1, 1), (512, 256, 1, 2)], "xb0")
-        new_diff(768, 256, 0, "diffB")
-        gather([(512, 256, 1, 3), (768, 256, 0, 0)], "xb1")
-        gather_table(0, "w2b1")
-        damping(0, "w2raw00")
-        damping(1, "w2raw01")
-        product(0)
-        gather([(768, 256, 0, 1), (768, 256, 0, 2)], "w2raw00")
-        prepare_x(A, 512, 256, 1, "xbB")
-        new_diff(768, 256, 1, "diffC")
-        gather([(768, 256, 0, 3), (768, 256, 1, 0)], "xbB")
-        damping(2, "w2raw10")
-        product(1)
-        gather_table(1, "w2raw01")
-        hidden(0, "AA", "hb0")
-        gather([(768, 256, 1, 1), (768, 256, 1, 2), (768, 256, 1, 3)], "hb0")
-        damping(3, "w2raw11")
-        product(2)
-        prepare_x(A, 768, 256, 0, "xb0")
-        hidden(1, "AA", "hb1")
-        prepare_x(V, 768, 256, 1, "xb1")
-        damping(4, "w2raw00")
-        product(3)
-        gather_table(2, "w2raw11")
-        scores(0, A)
-        hidden(2, "AA", "tab_s")
-        damping(5, "w2raw10")
-        product(4)
-        gather_table(3, "w2raw00")
-        scores(1, A)
-        hidden(3, "VV", "hb1")
-        damping(6, "w2raw01")
-        product(5)
-        scores(2, V)
-        hidden(4, "VV", "tab_s")
-        damping(7, "w2raw10", True)
-        product(6)
-        scores(3, V)
-        hidden(5, "VV", "hb1")
-        scores(4, A)
-        hidden(6, "AA", "tab_s")
-        product(7)
-        scores(5, A)
-        hidden(7, "AV", "hb1")
-        scores(6, A)
-        scores(7, A)
+        gather([(0, 256, 1, 3), (256, 256, 1, 3)], "cmp1")
+        prepare_x(A, 0, 256, 1, "xb2", 0)
+        prepare_x(A, 256, 256, 1, "xb3", 0)
+        new_diff(512, 512, 1, "diffA")
+        gather([(512, 512, 1, 0), (512, 512, 1, 1)], "xb2")
+        gather([(512, 512, 1, 2), (512, 512, 1, 3)], "diffC")
+        gather_table(0, 1024, "diffC")
+        damping(0, "w2raw00", ("e0", "e1"))
+        damping(1, "w2raw01", ("d0", "d1"))
+        damping(2, "w2raw10", ("e0", "e1"))
+        prepare_x(A, 512, 512, 1, "m0", 512)
+        damping(3, "w2raw11", ("d0", "d1"))
+        for jt in range(8):
+            if jt < 4:
+                damping(jt + 4, ("w2b1", "w2raw00", "w2raw01", "w2raw10")[jt], ("e0", "e1"), jt == 3)
+            product(jt, ("m0", "w2b0")[jt % 2])
+            if jt >= 1:
+                hidden(jt - 1, "VV" if jt < 6 else "AV", "hb%d" % (jt % 2))
+            if jt >= 2:
+                scores(jt - 2, V if jt < 5 else A, "res%d" % (jt % 2))
+        hidden(7, "AV", "hb0")
+        scores(6, A, "res0")
+        scores(7, A, "res1")

@@ -176,6 +176,51 @@ def tile_list_differential_star_photometry_kernel(
             for i in range(n // P):
                 x_q[lo // P + i, a] = (codes[:, P * i : P * (i + 1)], scales[:, P * i : P * (i + 1)])
 
+        picked = {}
+
+        def new_pick(side, lo, a, tag):
+            picked[side, lo, a] = sbuf([P, 4, 512], F32, tag)
+
+        def pick(side, lo, a, t):
+            dst = picked[side, lo, a][:, t, :]
+            cols = slice(lo // 16, (lo + 512) // 16)
+            if side == 0:
+                nc.vector.tensor_copy(dst, planes[a, t][:].indirect(idx2[:, cols]))
+            else:
+                nc.vector.tensor_scalar(dst, planes[a, t][:].indirect(idx3[:, cols]), -1.0, 0.0, ALU.mult, ALU.add)
+
+        def turn_x(base, lo, n, a, rows_tag, tag, banks):
+            rows = sbuf([P, n // P, 512], BF16, rows_tag)
+            rounded = sbuf([P, n, 4], BF16, tag)
+            for i in range(n // P):
+                cols = slice(lo - base + P * i, lo - base + P * (i + 1))
+                total = bank(banks[i])
+                for t in range(4):
+                    for side in range(2):
+                        nc.tensor.matmul(
+                            total[:, P * t : P * (t + 1)], picked[side, base, a][:, t, cols], ident[:],
+                            start=(t == 0 and side == 0), stop=(t == 3 and side == 1), is_transpose=True,
+                        )
+                nc.scalar.copy(
+                    rows[:, i, :].rearrange("j (u p e) -> j u p e", u=2, e=2),
+                    total[:].rearrange("j (u e p) -> j u p e", u=2, e=2),
+                )
+                if i % 2 == 0:
+                    back = bank(banks[i])
+                pairs = rows[:, i, :].bitcast(F32)
+                for u in range(2):
+                    at = P * (2 * (i % 2) + u)
+                    nc.tensor.transpose(back[:, at : at + P], pairs[:, P * u : P * (u + 1)], ident[:])
+                if i % 2 == 1:
+                    nc.scalar.copy(
+                        rounded[:, P * (i - 1) : P * (i + 1), :].rearrange("p j t -> p (j t)").bitcast(F32)
+                        .rearrange("p (i j u) -> p i j u", i=2, u=2),
+                        back[:].rearrange("p (i u j) -> p i j u", i=2, u=2),
+                    )
+            codes, scales = quantize(rounded[:].rearrange("p c t -> p (c t)"), n, "xq%d_%d" % (lo, a))
+            for i in range(n // P):
+                x_q[lo // P + i, a] = (codes[:, P * i : P * (i + 1)], scales[:, P * i : P * (i + 1)])
+
         def gather_table(lo, n, tag):
             words = sbuf([P, 2, n], U32, tag)
             for a in range(2):
@@ -204,7 +249,7 @@ def tile_list_differential_star_photometry_kernel(
                     e[:].rearrange("j (c i t) -> j c t i", t=4, i=4),
                     ACT.Square,
                 )
-            root = sbuf([P, 2, 512], F32, "m0" if jt == 2 else "root%d" % (jt % 2))
+            root = sbuf([P, 2, 512], F32, "m0" if jt == 3 else "root%d" % (jt % 2))
             damp[jt] = sbuf([P, 2, 512], F32, tag)
             parts = [slice(0, 1), slice(1, 2)] if split else [slice(0, 2)]
             for part in parts:
@@ -214,10 +259,10 @@ def tile_list_differential_star_photometry_kernel(
 
         damped = {}
 
-        def product(jt, tag):
+        def product(jt, tag, banks):
             both = sbuf([P, 2, 512], F32, tag)
             for half in range(2):
-                d = bank("d%d" % half)
+                d = bank(banks[half])
                 for a in range(2):
                     nc.tensor.matmul_mx(
                         d[:],
@@ -278,38 +323,44 @@ def tile_list_differential_star_photometry_kernel(
             eng(result[:].rearrange("p n j -> p (n j)"), acc[:])
             nc.sync.dma_start(out[:, jt * P : (jt + 1) * P].rearrange("(n p) j -> p n j", p=P), result[:])
 
-        new_diff(0, 1024, 0, "diffA")
-        new_diff(0, 512, 1, "diffC")
+        for lo, name in ((0, "lo"), (512, "hi")):
+            for side in range(2):
+                new_pick(side, lo, 0, "pick%d%s" % (side, name))
         for t in range(4):
-            gather([(0, 1024, 0, t)], "cmp%d" % (t % 2))
-        prepare_w2(0, 0)
-        prepare_w2(0, 1)
-        prepare_x(A, 0, 512, 0, "w2raw01", 0)
+            for lo in (0, 512):
+                for side in range(2):
+                    pick(side, lo, 0, t)
+            prepare_w2(t // 2, t % 2)
+        turn_x(0, 0, 512, 0, "w2raw00", "w2raw01", ("e0", "e1", "d0", "d1"))
+        turn_x(512, 512, 512, 0, "w2raw10", "w2raw11", ("o0", "o1", "turn0", "turn1"))
+        new_diff(0, 512, 1, "diffC")
         for t in range(3):
             gather([(0, 512, 1, t)], "cmp%d" % (t % 2))
-        prepare_w2(1, 0)
-        prepare_x(A, 512, 512, 0, "w2raw10", 0)
-        prepare_w2(1, 1)
         gather([(0, 256, 1, 3), (256, 256, 1, 3)], "cmp1")
-        prepare_x(A, 0, 256, 1, "xb2", 0)
+        prepare_x(A, 0, 256, 1, "pick0lo", 0)
         prepare_x(A, 256, 256, 1, "xb3", 0)
-        new_diff(512, 512, 1, "diffA")
-        gather([(512, 512, 1, 0), (512, 512, 1, 1)], "xb2")
+        gather_table(0, 512, "pick0lo")
+        new_diff(512, 512, 1, "pick1lo")
+        gather([(512, 512, 1, 0), (512, 512, 1, 1)], "xb3")
         gather([(512, 512, 1, 2), (512, 512, 1, 3)], "diffC")
-        gather_table(0, 1024, "diffC")
         damping(0, "w2raw00", ("e0", "e1"))
-        damping(1, "w2raw01", ("d0", "d1"))
+        damping(1, "w2raw01", ("o0", "o1"))
         damping(2, "w2raw10", ("e0", "e1"))
-        prepare_x(A, 512, 512, 1, "m0", 512)
-        damping(3, "w2raw11", ("d0", "d1"))
-        for jt in range(8):
-            if jt < 4:
-                damping(jt + 4, ("w2b1", "w2raw00", "w2raw01", "w2raw10")[jt], ("e0", "e1"), jt == 3)
-            product(jt, ("m0", "w2b0")[jt % 2])
-            if jt >= 1:
-                hidden(jt - 1, "VV" if jt < 6 else "AV", "hb%d" % (jt % 2))
+        damping(3, "w2raw11", ("turn0", "turn1"))
+        product(0, "diffC", ("d0", "d1"))
+        product(1, "xb3", ("o0", "o1"))
+        prepare_x(A, 512, 256, 1, "sq1", 512)
+        prepare_x(A, 768, 256, 1, "m0", 512)
+        for jt in range(1, 8):
+            if jt < 5:
+                damping(jt + 3, ("w2b1", "w2raw00", "w2raw01", "w2raw10")[jt - 1], ("e0", "e1"), jt == 4)
+            if jt > 1:
+                product(jt, ("w2b0", "xb3")[jt % 2], ("d0", "d1"))
+            hidden(jt - 1, "VV" if jt < 6 else "AV", ("cmp0", "m0")[jt % 2])
+            if jt == 2:
+                gather_table(512, 512, "pick1lo")
             if jt >= 2:
-                scores(jt - 2, V if jt < 5 else A, "res%d" % (jt % 2))
-        hidden(7, "AV", "hb0")
-        scores(6, A, "res0")
-        scores(7, A, "res1")
+                scores(jt - 2, V if jt < 5 else A, ("pick0hi", "pick1hi")[jt % 2])
+        hidden(7, "AV", "cmp0")
+        scores(6, A, "pick0hi")
+        scores(7, A, "pick1hi")

@@ -73,17 +73,19 @@ def tile_list_differential_star_photometry_kernel(
             )
 
         load_plane(0, 0)
+        load_plane(0, 1)
+        load_plane(0, 2)
         load_w2(0, 0)
         b_col = sbuf([P, 2, 4], F32, "b_col")
         nc.sync.dma_start(b_col[:], b.rearrange("(a p t) -> p a t", a=2, t=4))
-        load_plane(0, 1)
-        load_w2(0, 1)
-        load_plane(0, 2)
-        load_w2(1, 0)
         load_plane(0, 3)
+        load_plane(1, 0)
+        load_w2(0, 1)
+        load_plane(1, 1)
+        load_w2(1, 0)
+        load_plane(1, 2)
         load_w2(1, 1)
-        for t in range(4):
-            load_plane(1, t)
+        load_plane(1, 3)
         tab_w = []
 
         def load_table(a):
@@ -92,28 +94,28 @@ def tile_list_differential_star_photometry_kernel(
 
         def load_scales(plane, rows):
             for q in range(4):
-                nc.sync.dma_start(
+                nc.gpsimd.dma_start(
                     plane[32 * q : 32 * q + 4].bitcast(I32),
                     rows[:, 4 * q : 4 * q + 4, :].rearrange("a r n -> r a n").bitcast(I32),
                 )
 
         def move_scales(a):
             for q in range(4):
-                nc.sync.dma_start(
+                nc.gpsimd.dma_start(
                     v_s[32 * q : 32 * q + 4, a, :].bitcast(I32),
                     v_rows[16 * a + 4 * q : 16 * a + 4 * q + 4, :].bitcast(I32),
                 )
 
-        load_table(0)
         load_scales(w1_s, w1_scales)
-        load_table(1)
         move_scales(0)
+        move_scales(1)
+        load_scales(w3_s, w3_scales)
+        load_table(0)
+        load_table(1)
         w1_w = sbuf([P, 2, 2 * H], U8, "w1_w")
         nc.sync.dma_start(w1_w[:].bitcast(I32), w1_words.rearrange("a p n -> p a n").bitcast(I32))
-        move_scales(1)
         w3_w = sbuf([P, 2, N], U32, "w3_w")
         nc.sync.dma_start(w3_w[:].bitcast(I32), w3_words.rearrange("a p n i -> p a (n i)").bitcast(I32))
-        load_scales(w3_s, w3_scales)
 
 
         b_rows = sbuf([P, 2, 512], F32, "b_rows")
@@ -176,51 +178,6 @@ def tile_list_differential_star_photometry_kernel(
             for i in range(n // P):
                 x_q[lo // P + i, a] = (codes[:, P * i : P * (i + 1)], scales[:, P * i : P * (i + 1)])
 
-        picked = {}
-
-        def new_pick(side, lo, a, tag):
-            picked[side, lo, a] = sbuf([P, 4, 512], F32, tag)
-
-        def pick(side, lo, a, t):
-            dst = picked[side, lo, a][:, t, :]
-            cols = slice(lo // 16, (lo + 512) // 16)
-            if side == 0:
-                nc.vector.tensor_copy(dst, planes[a, t][:].indirect(idx2[:, cols]))
-            else:
-                nc.vector.tensor_scalar(dst, planes[a, t][:].indirect(idx3[:, cols]), -1.0, 0.0, ALU.mult, ALU.add)
-
-        def turn_x(base, lo, n, a, rows_tag, tag, banks):
-            rows = sbuf([P, n // P, 512], BF16, rows_tag)
-            rounded = sbuf([P, n, 4], BF16, tag)
-            for i in range(n // P):
-                cols = slice(lo - base + P * i, lo - base + P * (i + 1))
-                total = bank(banks[i])
-                for t in range(4):
-                    for side in range(2):
-                        nc.tensor.matmul(
-                            total[:, P * t : P * (t + 1)], picked[side, base, a][:, t, cols], ident[:],
-                            start=(t == 0 and side == 0), stop=(t == 3 and side == 1), is_transpose=True,
-                        )
-                nc.scalar.copy(
-                    rows[:, i, :].rearrange("j (u p e) -> j u p e", u=2, e=2),
-                    total[:].rearrange("j (u e p) -> j u p e", u=2, e=2),
-                )
-                if i % 2 == 0:
-                    back = bank(banks[i])
-                pairs = rows[:, i, :].bitcast(F32)
-                for u in range(2):
-                    at = P * (2 * (i % 2) + u)
-                    nc.tensor.transpose(back[:, at : at + P], pairs[:, P * u : P * (u + 1)], ident[:])
-                if i % 2 == 1:
-                    nc.scalar.copy(
-                        rounded[:, P * (i - 1) : P * (i + 1), :].rearrange("p j t -> p (j t)").bitcast(F32)
-                        .rearrange("p (i j u) -> p i j u", i=2, u=2),
-                        back[:].rearrange("p (i u j) -> p i j u", i=2, u=2),
-                    )
-            codes, scales = quantize(rounded[:].rearrange("p c t -> p (c t)"), n, "xq%d_%d" % (lo, a))
-            for i in range(n // P):
-                x_q[lo // P + i, a] = (codes[:, P * i : P * (i + 1)], scales[:, P * i : P * (i + 1)])
-
         def gather_table(lo, n, tag):
             words = sbuf([P, 2, n], U32, tag)
             for a in range(2):
@@ -230,7 +187,7 @@ def tile_list_differential_star_photometry_kernel(
 
         damp = {}
 
-        def damping(jt, tag, banks, split=False):
+        def damping(jt, tag, banks, root_tag, split=False):
             square = sbuf([P, 2, 512], F32, "sq%d" % (jt % 2))
             for half in range(2):
                 e = bank(banks[half])
@@ -249,7 +206,7 @@ def tile_list_differential_star_photometry_kernel(
                     e[:].rearrange("j (c i t) -> j c t i", t=4, i=4),
                     ACT.Square,
                 )
-            root = sbuf([P, 2, 512], F32, "m0" if jt == 3 else "root%d" % (jt % 2))
+            root = sbuf([P, 2, 512], F32, root_tag)
             damp[jt] = sbuf([P, 2, 512], F32, tag)
             parts = [slice(0, 1), slice(1, 2)] if split else [slice(0, 2)]
             for part in parts:
@@ -282,11 +239,12 @@ def tile_list_differential_star_photometry_kernel(
                 )
 
         h_q = {}
+        h_b = {}
 
-        def hidden(jt, engines, tag):
+        def hidden(jt, engines, tag, banks=("turn0", "turn1"), split=False):
             rounded = sbuf([P, 2, P, 4], BF16, tag)
             for half in range(2):
-                turned = bank("turn%d" % half)
+                turned = bank(banks[half])
                 on_scalar = engines[half] == "A"
                 if on_scalar:
                     for t in range(4):
@@ -304,7 +262,15 @@ def tile_list_differential_star_photometry_kernel(
                     nc.scalar.copy(rounded[:, half], view)
                 else:
                     nc.vector.tensor_tensor(rounded[:, half], view, b_rep[:, half], ALU.add)
-            h_q[jt] = quantize(rounded[:].rearrange("p a j t -> p (a j t)"), 2 * P, "hq%d" % (jt % 2))
+                if split:
+                    h_q[jt, half] = quantize(rounded[:, half].rearrange("p j t -> p (j t)"), P, "hq_last%d" % half)
+            h_b[jt] = rounded
+
+        def quantize_h(jt, codes_tag=None):
+            flat = h_b[jt][:].rearrange("p a j t -> p (a j t)")
+            codes, scales = quantize(flat, 2 * P, "hq%d" % (jt % 2), codes_tag)
+            for a in range(2):
+                h_q[jt, a] = (codes[:, P * a : P * (a + 1)], scales[:, P * a : P * (a + 1)])
 
         def scores(jt, eng, tag):
             acc = bank("o%d" % (jt % 2))
@@ -314,8 +280,8 @@ def tile_list_differential_star_photometry_kernel(
                         acc[:, P * nt : P * (nt + 1)],
                         lhsT=w3_w[:, a, P * nt : P * (nt + 1)].bitcast(FP8X4),
                         lhsT_scale=w3_s[:, a, P * nt : P * (nt + 1)],
-                        rhs=h_q[jt][0][:, P * a : P * (a + 1)].bitcast(FP8X4),
-                        rhs_scale=h_q[jt][1][:, P * a : P * (a + 1)],
+                        rhs=h_q[jt, a][0][:].bitcast(FP8X4),
+                        rhs_scale=h_q[jt, a][1][:],
                         start=(a == 0),
                         stop=(a == 1),
                     )
@@ -323,44 +289,91 @@ def tile_list_differential_star_photometry_kernel(
             eng(result[:].rearrange("p n j -> p (n j)"), acc[:])
             nc.sync.dma_start(out[:, jt * P : (jt + 1) * P].rearrange("(n p) j -> p n j", p=P), result[:])
 
-        for lo, name in ((0, "lo"), (512, "hi")):
-            for side in range(2):
-                new_pick(side, lo, 0, "pick%d%s" % (side, name))
-        for t in range(4):
-            for lo in (0, 512):
-                for side in range(2):
-                    pick(side, lo, 0, t)
-            prepare_w2(t // 2, t % 2)
-        turn_x(0, 0, 512, 0, "w2raw00", "w2raw01", ("e0", "e1", "d0", "d1"))
-        turn_x(512, 512, 512, 0, "w2raw10", "w2raw11", ("o0", "o1", "turn0", "turn1"))
+        def last_scores(jt, banks, tags):
+            accs = [bank(name) for name in banks]
+            for a in range(2):
+                for nt in range(4):
+                    nc.tensor.matmul_mx(
+                        accs[nt // 2][:, P * (nt % 2) : P * (nt % 2 + 1)],
+                        lhsT=w3_w[:, a, P * nt : P * (nt + 1)].bitcast(FP8X4),
+                        lhsT_scale=w3_s[:, a, P * nt : P * (nt + 1)],
+                        rhs=h_q[jt, a][0][:].bitcast(FP8X4),
+                        rhs_scale=h_q[jt, a][1][:],
+                        start=(a == 0 and nt % 2 == 0),
+                        stop=(a == 1 and nt % 2 == 1),
+                    )
+            for part, eng in enumerate((A, V)):
+                result = sbuf([P, 2, P], F32, tags[part])
+                eng(result[:].rearrange("p n j -> p (n j)"), accs[part][:, 0 : 2 * P])
+                nc.sync.dma_start(
+                    out[256 * part : 256 * (part + 1), jt * P : (jt + 1) * P].rearrange("(n p) j -> p n j", p=P),
+                    result[:],
+                )
+
+        new_diff(0, 512, 0, "diffA")
         new_diff(0, 512, 1, "diffC")
+        for t in range(4):
+            gather([(0, 512, 0, t)], "cmp%d" % (t % 2))
+        prepare_w2(0, 0)
+        prepare_x(A, 0, 512, 0, "xb0", 0)
         for t in range(3):
             gather([(0, 512, 1, t)], "cmp%d" % (t % 2))
+            prepare_w2((t + 1) // 2, (t + 1) % 2)
         gather([(0, 256, 1, 3), (256, 256, 1, 3)], "cmp1")
-        prepare_x(A, 0, 256, 1, "pick0lo", 0)
+        prepare_x(A, 0, 256, 1, "xb2", 0)
         prepare_x(A, 256, 256, 1, "xb3", 0)
-        gather_table(0, 512, "pick0lo")
-        new_diff(512, 512, 1, "pick1lo")
-        gather([(512, 512, 1, 0), (512, 512, 1, 1)], "xb3")
-        gather([(512, 512, 1, 2), (512, 512, 1, 3)], "diffC")
-        damping(0, "w2raw00", ("e0", "e1"))
-        damping(1, "w2raw01", ("o0", "o1"))
-        damping(2, "w2raw10", ("e0", "e1"))
-        damping(3, "w2raw11", ("turn0", "turn1"))
-        product(0, "diffC", ("d0", "d1"))
-        product(1, "xb3", ("o0", "o1"))
-        prepare_x(A, 512, 256, 1, "sq1", 512)
-        prepare_x(A, 768, 256, 1, "m0", 512)
-        for jt in range(1, 8):
-            if jt < 5:
-                damping(jt + 3, ("w2b1", "w2raw00", "w2raw01", "w2raw10")[jt - 1], ("e0", "e1"), jt == 4)
-            if jt > 1:
-                product(jt, ("w2b0", "xb3")[jt % 2], ("d0", "d1"))
-            hidden(jt - 1, "VV" if jt < 6 else "AV", ("cmp0", "m0")[jt % 2])
-            if jt == 2:
-                gather_table(512, 512, "pick1lo")
-            if jt >= 2:
-                scores(jt - 2, V if jt < 5 else A, ("pick0hi", "pick1hi")[jt % 2])
-        hidden(7, "AV", "cmp0")
-        scores(6, A, "pick0hi")
-        scores(7, A, "pick1hi")
+        D = ("d0", "d1")
+        E = ("e0", "e1")
+        new_diff(512, 256, 0, "diffA")
+        gather([(512, 256, 0, 0), (512, 256, 0, 1)], "xb2")
+        gather_table(0, 512, "w2b1")
+        gather([(512, 256, 0, 2), (512, 256, 0, 3)], "xb3")
+        damping(0, "w2raw00", E, "root0")
+        damping(1, "w2raw01", D, "root1", True)
+        prepare_x(A, 512, 256, 0, "root1", 512)
+        damping(2, "w2raw10", ("o0", "o1"), "root2", True)
+        product(0, "m0", D)
+        new_diff(512, 512, 1, "diffC")
+        gather([(512, 256, 1, t) for t in range(4)], "w2raw00")
+        product(1, "w2b0", D)
+        hidden(0, "AA", "root0")
+        prepare_x(A, 512, 256, 1, "root2", 512)
+        new_diff(768, 256, 0, "diffA")
+        gather([(768, 256, 0, t) for t in range(4)], "root2")
+        damping(3, "w2raw11", E, "root3", True)
+        quantize_h(0)
+        hidden(1, "AA", "root3")
+        product(2, "root2", D)
+        gather([(768, 256, 1, t) for t in range(4)], "w2raw10")
+        damping(4, "w2raw00", E, "root1", True)
+        prepare_x(A, 768, 256, 0, "root1", 768)
+        quantize_h(1)
+        scores(0, A, "res0")
+        hidden(2, "AA", "xb2")
+        product(3, "w2raw10", D)
+        quantize_h(2)
+        prepare_x(A, 768, 256, 1, "xb3", 512)
+        gather_table(512, 512, "xb3")
+        damping(5, "w2raw01", E, "root0", True)
+        hidden(3, "AA", "hb1")
+        quantize_h(3)
+        damping(6, "w2raw10", E, "root1", True)
+        scores(1, V, "res1")
+        product(4, "m0", D)
+        product(5, "w2b0", D)
+        scores(2, A, "res0")
+        damping(7, "w2raw00", E, "root2", True)
+        hidden(4, "VV", "xb2")
+        quantize_h(4)
+        product(6, "m0", D)
+        scores(3, A, "res1")
+        hidden(5, "VV", "hb1")
+        quantize_h(5)
+        product(7, "w2b0", E)
+        scores(4, A, "res0")
+        hidden(6, "AV", "xb2", D)
+        quantize_h(6)
+        scores(5, A, "res1")
+        hidden(7, "AV", "hb1", split=True)
+        scores(6, A, "res0")
+        last_scores(7, E, ("diffC", "cmp1"))

@@ -312,8 +312,9 @@ def tile_list_differential_star_photometry_kernel(
 
         new_diff(0, 512, 0, "diffA")
         new_diff(0, 512, 1, "diffC")
+        new_diff(512, 256, 0, "diffB")
         for t in range(4):
-            gather([(0, 512, 0, t)], "cmp%d" % (t % 2))
+            gather([(0, 512, 0, t)] + ([(512, 256, 0, t)] if t < 2 else []), "cmp%d" % (t % 2))
         prepare_w2(0, 0)
         prepare_x(A, 0, 512, 0, "xb0", 0)
         for t in range(3):
@@ -324,20 +325,19 @@ def tile_list_differential_star_photometry_kernel(
         prepare_x(A, 256, 256, 1, "xb3", 0)
         D = ("d0", "d1")
         E = ("e0", "e1")
-        new_diff(512, 256, 0, "diffA")
-        gather([(512, 256, 0, 0), (512, 256, 0, 1)], "xb2")
+        gather([(512, 256, 0, 2), (512, 256, 0, 3)], "xb2")
         gather_table(0, 512, "w2b1")
-        gather([(512, 256, 0, 2), (512, 256, 0, 3)], "xb3")
+        new_diff(512, 512, 1, "diffC")
+        gather([(512, 256, 1, 0), (512, 256, 1, 1)], "xb3")
         damping(0, "w2raw00", E, "root0")
         damping(1, "w2raw01", D, "root1", True)
         prepare_x(A, 512, 256, 0, "root1", 512)
         damping(2, "w2raw10", ("o0", "o1"), "root2", True)
         product(0, "m0", D)
-        new_diff(512, 512, 1, "diffC")
-        gather([(512, 256, 1, t) for t in range(4)], "w2raw00")
+        gather([(512, 256, 1, 2), (512, 256, 1, 3)], "w2raw00")
         product(1, "w2b0", D)
-        hidden(0, "AA", "root0")
         prepare_x(A, 512, 256, 1, "root2", 512)
+        hidden(0, "AA", "root0")
         new_diff(768, 256, 0, "diffA")
         gather([(768, 256, 0, t) for t in range(4)], "root2")
         damping(3, "w2raw11", E, "root3", True)
@@ -355,7 +355,7 @@ def tile_list_differential_star_photometry_kernel(
         prepare_x(A, 768, 256, 1, "xb3", 512)
         gather_table(512, 512, "xb3")
         damping(5, "w2raw01", E, "root0", True)
-        hidden(3, "AA", "hb1")
+        hidden(3, "AA", "tab_s")
         quantize_h(3)
         damping(6, "w2raw10", E, "root1", True)
         scores(1, V, "res1")
@@ -367,13 +367,13 @@ def tile_list_differential_star_photometry_kernel(
         quantize_h(4)
         product(6, "m0", D)
         scores(3, A, "res1")
-        hidden(5, "VV", "hb1")
+        hidden(5, "VV", "tab_s")
         quantize_h(5)
         product(7, "w2b0", E)
         scores(4, A, "res0")
         hidden(6, "AV", "xb2", D)
         quantize_h(6)
         scores(5, A, "res1")
-        hidden(7, "AV", "hb1", split=True)
+        hidden(7, "AV", "tab_s", split=True)
         scores(6, A, "res0")
         last_scores(7, E, ("diffC", "cmp1"))

@@ -18,8 +18,9 @@ ACT = mybir.ActivationFunctionType
 ALU = mybir.AluOpType
 
 P = 128
-CW = 256
-TILES = S // P
+WHOLE = (slice(0, 2),)
+HALVES = (slice(0, 1), slice(1, 2))
+PAIRS = ()
 
 
 def tile_list_differential_star_photometry_kernel(
@@ -60,6 +61,7 @@ def tile_list_differential_star_photometry_kernel(
 
         planes = {}
         w2_raw = {}
+        tab_w = {}
 
         def load_plane(a, t):
             planes[a, t] = sbuf([P, T], F32, "plane%d%d" % (a, t))
@@ -72,24 +74,8 @@ def tile_list_differential_star_photometry_kernel(
                 w2[512 * a : 512 * (a + 1), 512 * half : 512 * (half + 1)].rearrange("(p t) c -> p t c", t=4),
             )
 
-        load_plane(0, 0)
-        load_plane(0, 1)
-        load_plane(0, 2)
-        load_w2(0, 0)
-        b_col = sbuf([P, 2, 4], F32, "b_col")
-        nc.sync.dma_start(b_col[:], b.rearrange("(a p t) -> p a t", a=2, t=4))
-        load_plane(0, 3)
-        load_plane(1, 0)
-        load_w2(0, 1)
-        load_plane(1, 1)
-        load_w2(1, 0)
-        load_plane(1, 2)
-        load_w2(1, 1)
-        load_plane(1, 3)
-        tab_w = []
-
-        def load_table(a):
-            tab_w.append(sbuf([P, T], U32, "tab_w%d" % a))
+        def load_table(a, tag):
+            tab_w[a] = sbuf([P, T], U32, tag)
             nc.sync.dma_start(tab_w[a][:].bitcast(I32), tab_words[a].rearrange("p n i -> p (n i)").bitcast(I32))
 
         def load_scales(plane, rows):
@@ -106,75 +92,72 @@ def tile_list_differential_star_photometry_kernel(
                     v_rows[16 * a + 4 * q : 16 * a + 4 * q + 4, :].bitcast(I32),
                 )
 
-        load_scales(w1_s, w1_scales)
-        move_scales(0)
-        move_scales(1)
-        load_scales(w3_s, w3_scales)
-        load_table(0)
-        load_table(1)
-        w1_w = sbuf([P, 2, 2 * H], U8, "w1_w")
-        nc.sync.dma_start(w1_w[:].bitcast(I32), w1_words.rearrange("a p n -> p a n").bitcast(I32))
-        w3_w = sbuf([P, 2, N], U32, "w3_w")
-        nc.sync.dma_start(w3_w[:].bitcast(I32), w3_words.rearrange("a p n i -> p a (n i)").bitcast(I32))
-
-
-        b_rows = sbuf([P, 2, 512], F32, "b_rows")
-        for a in range(2):
-            spread = bank("turn%d" % a)
-            for t in range(4):
-                nc.tensor.transpose(
-                    spread[:, P * t : P * (t + 1)], b_col[:, a, t : t + 1].to_broadcast([P, P]), ident[:]
-                )
-            nc.scalar.copy(b_rows[:, a, :], spread[:])
-
-        b_rep = sbuf([P, 2, P, 4], F32, "b_rep")
-        for a in range(2):
-            nc.scalar.copy(b_rep[:, a], b_col[:, a : a + 1, :].to_broadcast([P, P, 4]))
-
         A = nc.scalar.copy
         V = nc.vector.tensor_copy
+
+        def GS(dst, src):
+            nc.gpsimd.tensor_scalar(dst, src, 1.0, 0.0, ALU.mult, ALU.add)
 
         def interleave(eng, dst, src):
             eng(dst.rearrange("p (c i) t -> p c t i", i=4), src.rearrange("p t (c i) -> p c t i", i=4))
 
-        def quantize(src, width, tag, codes_tag=None):
-            codes = sbuf([P, width], U32, codes_tag or tag + "_c")
+        def quantize(src, width, tag, codes=None):
+            if codes is None:
+                codes = sbuf([P, width], U32, tag + "_c")[:]
             scales = sbuf([P, width], U8, tag + "_s")
-            nc.vector.quantize_mx(out=codes[:].bitcast(FP8X4), scales=scales[:], in_=src)
-            return codes, scales
+            nc.vector.quantize_mx(out=codes.bitcast(FP8X4), scales=scales[:], in_=src)
+            return codes, scales[:]
 
+        w2_b = {}
         w2_q = {}
 
-        def prepare_w2(half, a):
-            rounded = sbuf([P, 512, 4], BF16, "w2b%d" % a)
-            interleave(A, rounded[:], w2_raw[half, a][:])
-            w2_q[half, a] = quantize(rounded[:].rearrange("p c t -> p (c t)"), 512, "w2q%d%d" % (half, a))
+        def round_w2(half, a, tag):
+            w2_b[half, a] = sbuf([P, 512, 4], BF16, tag)
+            interleave(A, w2_b[half, a][:], w2_raw[half, a][:])
+
+        def quantize_w2(half, a, codes=None):
+            w2_q[half, a] = quantize(
+                w2_b[half, a][:].rearrange("p c t -> p (c t)"), 512, "w2q%d%d" % (half, a), codes
+            )
 
         diff = {}
+        other = {}
+        x_b = {}
         x_q = {}
         v_w = {}
 
-        def gather(units, tag):
-            comparison = sbuf([P, sum(u[1] for u in units)], F32, tag)
-            at = [sum(u[1] for u in units[:i]) for i in range(len(units))]
-            for c0, (lo, n, a, t) in zip(at, units):
-                nc.vector.tensor_copy(
-                    comparison[:, c0 : c0 + n], planes[a, t][:].indirect(idx3[:, lo // 16 : (lo + n) // 16])
-                )
-            for c0, (lo, n, a, t) in zip(at, units):
-                base = max(k for k, pas in diff if pas == a and k <= lo)
-                nc.vector.tensor_tensor(
-                    diff[base, a][:, t, lo - base : lo - base + n], planes[a, t][:].indirect(idx2[:, lo // 16 : (lo + n) // 16]),
-                    comparison[:, c0 : c0 + n], ALU.subtract,
-                )
-
         def new_diff(lo, n, a, tag):
-            diff[lo, a] = sbuf([P, 4, n], F32, tag)
+            tile = sbuf([P, 4, n], F32, tag)
+            for at in range(0, n, P):
+                diff[lo + at, a] = (tile, at)
 
-        def prepare_x(eng, lo, n, a, tag, base, codes_tag=None):
-            rounded = sbuf([P, n, 4], BF16, tag)
-            interleave(eng, rounded[:], diff[base, a][:, :, lo - base : lo - base + n])
-            codes, scales = quantize(rounded[:].rearrange("p c t -> p (c t)"), n, "xq%d_%d" % (lo, a), codes_tag)
+        def pick(units, tag):
+            tile = sbuf([P, sum(u[1] for u in units)], F32, tag)
+            at = 0
+            for lo, n, a, t in units:
+                other[lo, n, a, t] = tile[:, at : at + n]
+                nc.vector.tensor_copy(
+                    other[lo, n, a, t], planes[a, t][:].indirect(idx3[:, lo // 16 : (lo + n) // 16])
+                )
+                at = at + n
+
+        def subtract(units):
+            for lo, n, a, t in units:
+                tile, at = diff[lo, a]
+                nc.vector.tensor_tensor(
+                    tile[:, t, at : at + n], planes[a, t][:].indirect(idx2[:, lo // 16 : (lo + n) // 16]),
+                    other[lo, n, a, t], ALU.subtract,
+                )
+
+        def round_x(eng, lo, n, a, tag):
+            tile, at = diff[lo, a]
+            x_b[lo, a] = sbuf([P, n, 4], BF16, tag)
+            interleave(eng, x_b[lo, a][:], tile[:, :, at : at + n])
+
+        def quantize_x(lo, n, a, codes=None):
+            codes, scales = quantize(
+                x_b[lo, a][:].rearrange("p c t -> p (c t)"), n, "xq%d_%d" % (lo, a), codes
+            )
             for i in range(n // P):
                 x_q[lo // P + i, a] = (codes[:, P * i : P * (i + 1)], scales[:, P * i : P * (i + 1)])
 
@@ -185,41 +168,71 @@ def tile_list_differential_star_photometry_kernel(
                 for i in range(n // P):
                     v_w[lo // P + i, a] = words[:, a, P * i : P * (i + 1)]
 
+        def pairs_out(ap):
+            return ap.rearrange("j (u p e) -> j u p e", u=2, e=2)
+
+        def pairs_in(ap):
+            return ap.rearrange("j (p u e) -> j u p e", u=2, e=2)
+
+        def quads_out(ap):
+            return ap.rearrange("j (t c i) -> j c t i", t=4, i=4)
+
+        def quads_in(ap):
+            return ap.rearrange("j (c i t) -> j c t i", t=4, i=4)
+
+        def walk_out(jt, ap):
+            return pairs_out(ap) if jt in PAIRS else quads_out(ap)
+
+        def walk_in(jt, ap):
+            return pairs_in(ap) if jt in PAIRS else quads_in(ap)
+
         damp = {}
 
-        def damping(jt, tag, banks, root_tag, split=False):
-            square = sbuf([P, 2, 512], F32, "sq%d" % (jt % 2))
-            for half in range(2):
+        square = {}
+        root = {}
+
+        e_bank = {}
+        d_bank = {}
+
+        def deviation(jt, banks, halves=(0, 1), passes=(1, 0)):
+            for half in halves:
                 e = bank(banks[half])
-                for a in range(2):
+                e_bank[jt, half] = e
+                for a in passes:
                     nc.tensor.matmul_mx(
                         e[:],
                         lhsT=x_q[jt, a][0].bitcast(FP8X4),
                         lhsT_scale=x_q[jt, a][1],
-                        rhs=w2_q[half, a][0][:].bitcast(FP8X4),
-                        rhs_scale=w2_q[half, a][1][:],
-                        start=(a == 0),
-                        stop=(a == 1),
+                        rhs=w2_q[half, a][0].bitcast(FP8X4),
+                        rhs_scale=w2_q[half, a][1],
+                        start=(a == passes[0]),
+                        stop=(a == passes[1]),
                     )
-                nc.scalar.activation(
-                    square[:, half, :].rearrange("j (t c i) -> j c t i", t=4, i=4),
-                    e[:].rearrange("j (c i t) -> j c t i", t=4, i=4),
-                    ACT.Square,
-                )
-            root = sbuf([P, 2, 512], F32, root_tag)
-            damp[jt] = sbuf([P, 2, 512], F32, tag)
-            parts = [slice(0, 1), slice(1, 2)] if split else [slice(0, 2)]
+
+        def squares(jt, tag, halves=(0, 1)):
+            if 0 in halves:
+                square[jt] = sbuf([P, 2, 512], F32, tag)
+            for half in halves:
+                nc.scalar.activation(walk_out(jt, square[jt][:, half, :]), walk_in(jt, e_bank[jt, half][:]), ACT.Square)
+
+        def roots(jt, tag, parts=WHOLE):
+            if parts[0].start == 0:
+                root[jt] = sbuf([P, 2, 512], F32, tag)
             for part in parts:
-                nc.scalar.activation(root[:, part], square[:, part], ACT.Abs_reciprocal_sqrt, bias=1.0)
+                nc.scalar.activation(root[jt][:, part], square[jt][:, part], ACT.Abs_reciprocal_sqrt, bias=1.0)
+
+        def factor(jt, tag, parts=WHOLE):
+            if parts[0].start == 0:
+                damp[jt] = sbuf([P, 2, 512], F32, tag)
             for part in parts:
-                nc.scalar.activation(damp[jt][:, part], root[:, part], ACT.Square)
+                nc.scalar.activation(damp[jt][:, part], root[jt][:, part], ACT.Square)
 
         damped = {}
 
-        def product(jt, tag, banks):
-            both = sbuf([P, 2, 512], F32, tag)
+        def response(jt, banks):
             for half in range(2):
                 d = bank(banks[half])
+                d_bank[jt, half] = d
                 for a in range(2):
                     nc.tensor.matmul_mx(
                         d[:],
@@ -230,63 +243,94 @@ def tile_list_differential_star_photometry_kernel(
                         start=(a == 0),
                         stop=(a == 1),
                     )
-                damped[jt, half] = both[:, half, :]
+
+        def product(jt, tile):
+            damped[jt] = tile
+            for half in range(2):
                 nc.vector.tensor_tensor(
-                    damped[jt, half].rearrange("j (t c i) -> j c t i", t=4, i=4),
-                    d[:].rearrange("j (c i t) -> j c t i", t=4, i=4),
-                    damp[jt][:, half, :].rearrange("j (t c i) -> j c t i", t=4, i=4),
-                    ALU.mult,
+                    walk_out(jt, damped[jt][:, half, :]), walk_in(jt, d_bank[jt, half][:]),
+                    walk_out(jt, damp[jt][:, half, :]), ALU.mult,
                 )
 
-        h_q = {}
+        h_rows = {}
         h_b = {}
+        h_q = {}
 
-        def hidden(jt, engines, tag, banks=("turn0", "turn1"), split=False):
-            rounded = sbuf([P, 2, P, 4], BF16, tag)
+        turned = {}
+
+        def turn(jt, banks):
+            words = h_rows[jt][:].bitcast(F32)
+            per = 2 // len(banks)
+            turned[jt] = [bank(name) for name in banks]
             for half in range(2):
-                turned = bank(banks[half])
-                on_scalar = engines[half] == "A"
-                if on_scalar:
+                for u in range(2):
+                    i = 2 * (half % per) + u
+                    nc.tensor.transpose(
+                        turned[jt][half // per][:, P * i : P * (i + 1)], words[:, half, P * u : P * (u + 1)], ident[:]
+                    )
+
+        def spread_bias(jt, engines, banks):
+            turned[jt] = [bank(name) for name in banks]
+            for half in range(2):
+                if engines[half] == "A":
                     for t in range(4):
                         nc.tensor.matmul(
-                            turned[:, P * t : P * (t + 1)], b_rows[:, half, P * t : P * (t + 1)], ident[:],
+                            turned[jt][half][:, P * t : P * (t + 1)], b_quads[:, half, P * t : P * (t + 1)], ident[:],
                             start=(t == 0), stop=False, is_transpose=True,
                         )
+
+        def turn_floats(jt, engines):
+            for half in range(2):
                 for t in range(4):
                     nc.tensor.matmul(
-                        turned[:, P * t : P * (t + 1)], damped[jt, half][:, P * t : P * (t + 1)], ident[:],
-                        start=(t == 0 and not on_scalar), stop=(t == 3), is_transpose=True,
+                        turned[jt][half][:, P * t : P * (t + 1)], damped[jt][:, half, P * t : P * (t + 1)], ident[:],
+                        start=(t == 0 and engines[half] != "A"), stop=(t == 3), is_transpose=True,
                     )
-                view = turned[:].rearrange("p (t j) -> p j t", t=4)
-                if on_scalar:
-                    nc.scalar.copy(rounded[:, half], view)
+
+        def empty(jt, engines, tile):
+            h_b[jt] = tile
+            for half in range(2):
+                view = turned[jt][half][:].rearrange("p (t j) -> p j t", t=4)
+                if engines[half] == "A":
+                    nc.scalar.copy(tile[:, half], view)
                 else:
-                    nc.vector.tensor_tensor(rounded[:, half], view, b_rep[:, half], ALU.add)
-                if split:
-                    h_q[jt, half] = quantize(rounded[:, half].rearrange("p j t -> p (j t)"), P, "hq_last%d" % half)
-            h_b[jt] = rounded
+                    nc.vector.tensor_tensor(tile[:, half], view, b_rep[:, half], ALU.add)
 
-        def quantize_h(jt, codes_tag=None):
-            flat = h_b[jt][:].rearrange("p a j t -> p (a j t)")
-            codes, scales = quantize(flat, 2 * P, "hq%d" % (jt % 2), codes_tag)
-            for a in range(2):
-                h_q[jt, a] = (codes[:, P * a : P * (a + 1)], scales[:, P * a : P * (a + 1)])
+        def m_tile(tag):
+            return sbuf([P, 2, 512], F32, tag)[:]
 
-        def scores(jt, eng, tag):
-            acc = bank("o%d" % (jt % 2))
+        def h_tile(tag):
+            return sbuf([P, 2, P, 4], BF16, tag)[:]
+
+        def quantize_h(jt, tag, split=False):
+            if split:
+                for a in range(2):
+                    h_q[jt, a] = quantize(h_b[jt][:, a].rearrange("p j t -> p (j t)"), P, "%s%d" % (tag, a))
+            else:
+                codes, scales = quantize(h_b[jt].rearrange("p a j t -> p (a j t)"), 2 * P, tag)
+                for a in range(2):
+                    h_q[jt, a] = (codes[:, P * a : P * (a + 1)], scales[:, P * a : P * (a + 1)])
+
+        o_bank = {}
+
+        def scores(jt, name):
+            acc = bank(name)
+            o_bank[jt] = acc
             for nt in range(4):
                 for a in range(2):
                     nc.tensor.matmul_mx(
                         acc[:, P * nt : P * (nt + 1)],
                         lhsT=w3_w[:, a, P * nt : P * (nt + 1)].bitcast(FP8X4),
                         lhsT_scale=w3_s[:, a, P * nt : P * (nt + 1)],
-                        rhs=h_q[jt, a][0][:].bitcast(FP8X4),
-                        rhs_scale=h_q[jt, a][1][:],
+                        rhs=h_q[jt, a][0].bitcast(FP8X4),
+                        rhs_scale=h_q[jt, a][1],
                         start=(a == 0),
                         stop=(a == 1),
                     )
+
+        def store(jt, eng, tag):
             result = sbuf([P, 4, P], F32, tag)
-            eng(result[:].rearrange("p n j -> p (n j)"), acc[:])
+            eng(result[:].rearrange("p n j -> p (n j)"), o_bank[jt][:])
             nc.sync.dma_start(out[:, jt * P : (jt + 1) * P].rearrange("(n p) j -> p n j", p=P), result[:])
 
         def last_scores(jt, banks, tags):
@@ -297,8 +341,8 @@ def tile_list_differential_star_photometry_kernel(
                         accs[nt // 2][:, P * (nt % 2) : P * (nt % 2 + 1)],
                         lhsT=w3_w[:, a, P * nt : P * (nt + 1)].bitcast(FP8X4),
                         lhsT_scale=w3_s[:, a, P * nt : P * (nt + 1)],
-                        rhs=h_q[jt, a][0][:].bitcast(FP8X4),
-                        rhs_scale=h_q[jt, a][1][:],
+                        rhs=h_q[jt, a][0].bitcast(FP8X4),
+                        rhs_scale=h_q[jt, a][1],
                         start=(a == 0 and nt % 2 == 0),
                         stop=(a == 1 and nt % 2 == 1),
                     )
@@ -310,70 +354,198 @@ def tile_list_differential_star_photometry_kernel(
                     result[:],
                 )
 
-        new_diff(0, 512, 0, "diffA")
-        new_diff(0, 512, 1, "diffC")
-        new_diff(512, 256, 0, "diffB")
-        for t in range(4):
-            gather([(0, 512, 0, t)] + ([(512, 256, 0, t)] if t < 2 else []), "cmp%d" % (t % 2))
-        prepare_w2(0, 0)
-        prepare_x(A, 0, 512, 0, "xb0", 0)
-        for t in range(3):
-            gather([(0, 512, 1, t)], "cmp%d" % (t % 2))
-            prepare_w2((t + 1) // 2, (t + 1) % 2)
-        gather([(0, 256, 1, 3), (256, 256, 1, 3)], "cmp1")
-        prepare_x(A, 0, 256, 1, "xb2", 0)
-        prepare_x(A, 256, 256, 1, "xb3", 0)
-        D = ("d0", "d1")
+        G = nc.gpsimd
+        DA = ("d0", "d1")
+        DB = ("d2", "d3")
         E = ("e0", "e1")
-        gather([(512, 256, 0, 2), (512, 256, 0, 3)], "xb2")
-        gather_table(0, 512, "w2b1")
-        new_diff(512, 512, 1, "diffC")
-        gather([(512, 256, 1, 0), (512, 256, 1, 1)], "xb3")
-        damping(0, "w2raw00", E, "root0")
-        damping(1, "w2raw01", D, "root1", True)
-        prepare_x(A, 512, 256, 0, "root1", 512)
-        damping(2, "w2raw10", ("o0", "o1"), "root2", True)
-        product(0, "m0", D)
-        gather([(512, 256, 1, 2), (512, 256, 1, 3)], "w2raw00")
-        product(1, "w2b0", D)
-        prepare_x(A, 512, 256, 1, "root2", 512)
-        hidden(0, "AA", "root0")
-        new_diff(768, 256, 0, "diffA")
-        gather([(768, 256, 0, t) for t in range(4)], "root2")
-        damping(3, "w2raw11", E, "root3", True)
-        quantize_h(0)
-        hidden(1, "AA", "root3")
-        product(2, "root2", D)
-        gather([(768, 256, 1, t) for t in range(4)], "w2raw10")
-        damping(4, "w2raw00", E, "root1", True)
-        prepare_x(A, 768, 256, 0, "root1", 768)
-        quantize_h(1)
-        scores(0, A, "res0")
-        hidden(2, "AA", "xb2")
-        product(3, "w2raw10", D)
-        quantize_h(2)
-        prepare_x(A, 768, 256, 1, "xb3", 512)
-        gather_table(512, 512, "xb3")
-        damping(5, "w2raw01", E, "root0", True)
-        hidden(3, "AA", "tab_s")
-        quantize_h(3)
-        damping(6, "w2raw10", E, "root1", True)
-        scores(1, V, "res1")
-        product(4, "m0", D)
-        product(5, "w2b0", D)
-        scores(2, A, "res0")
-        damping(7, "w2raw00", E, "root2", True)
-        hidden(4, "VV", "xb2")
-        quantize_h(4)
-        product(6, "m0", D)
-        scores(3, A, "res1")
-        hidden(5, "VV", "tab_s")
-        quantize_h(5)
-        product(7, "w2b0", E)
-        scores(4, A, "res0")
-        hidden(6, "AV", "xb2", D)
-        quantize_h(6)
-        scores(5, A, "res1")
-        hidden(7, "AV", "tab_s", split=True)
-        scores(6, A, "res0")
-        last_scores(7, E, ("diffC", "cmp1"))
+
+        def chunk(lo, a):
+            return [(lo, 256, a, t) for t in range(4)]
+
+        load_plane(0, 0)
+        b_col = sbuf([P, 2, 4], F32, "b_col")
+        nc.sync.dma_start(b_col[:], b.rearrange("(a p t) -> p a t", a=2, t=4))
+        for t in range(1, 4):
+            load_plane(0, t)
+        load_w2(0, 0)
+        load_w2(0, 1)
+        load_w2(1, 0)
+        for t in range(4):
+            load_plane(1, t)
+        load_w2(1, 1)
+        load_scales(w1_s, w1_scales)
+        move_scales(0)
+        move_scales(1)
+        load_scales(w3_s, w3_scales)
+
+        b_quads = sbuf([P, 2, 512], F32, "b_quads")
+        for a in range(2):
+            spread = bank(DB[a])
+            for t in range(4):
+                nc.tensor.transpose(
+                    spread[:, P * t : P * (t + 1)], b_col[:, a, t : t + 1].to_broadcast([P, P]), ident[:]
+                )
+            nc.scalar.copy(b_quads[:, a, :], spread[:])
+        b_rep = sbuf([P, 2, P, 4], F32, "b_rep")
+        for a in range(2):
+            nc.scalar.copy(b_rep[:, a], b_col[:, a : a + 1, :].to_broadcast([P, P, 4]))
+
+        OO = ("turn", "o")
+        P3 = "VV"
+        P4 = "VV"
+        P5 = "AA"
+        P6 = "AV"
+        new_diff(0, 1024, 0, "diffA")
+        for t in range(4):
+            units = [(0, 512, 0, t), (512, 512, 0, t)]
+            pick(units, "cmp%d" % (t % 2))
+            subtract(units)
+        load_table(0, "plane00")
+        load_table(1, "plane01")
+        w1_w = sbuf([P, 2, 2 * H], U8, "w1_w")
+        nc.sync.dma_start(w1_w[:].bitcast(I32), w1_words.rearrange("a p n -> p a n").bitcast(I32))
+        w3_w = sbuf([P, 2, N], U32, "w3_w")
+        nc.sync.dma_start(w3_w[:].bitcast(I32), w3_words.rearrange("a p n i -> p a (n i)").bitcast(I32))
+        round_w2(0, 0, "w2b0")
+        quantize_w2(0, 0)
+        round_w2(0, 1, "w2b1")
+        quantize_w2(0, 1)
+        round_w2(1, 0, "w2b2")
+        round_x(A, 0, 512, 0, "w2raw01")
+        round_x(A, 512, 512, 0, "w2raw10")
+        new_diff(0, 256, 1, "diffB")
+        pick(chunk(0, 1)[0:2], "cmp0")
+        subtract(chunk(0, 1)[0:2])
+        pick(chunk(0, 1)[2:4], "plane02")
+        subtract(chunk(0, 1)[2:4])
+        round_x(A, 0, 256, 1, "xb0")
+        round_w2(1, 1, "w2b3")
+        late = sbuf([P, 3, 512], U32, "plane02")
+        quantize_x(0, 512, 0, late[:, 0])
+        quantize_w2(1, 0, late[:, 1])
+        quantize_x(512, 512, 0, late[:, 2])
+        quantize_x(0, 256, 1)
+        deviation(0, E, (0,), (0, 1))
+        deviation(1, OO, (0,), (0, 1))
+        squares(0, "sq0", (0,))
+        squares(1, "sq1", (0,))
+        new_diff(256, 256, 1, "w2raw11")
+        pick(chunk(256, 1)[0:2], "diffB")
+        pick(chunk(256, 1)[2:4], "xb0")
+        quantize_w2(1, 1)
+        deviation(0, E, (1,))
+        deviation(1, OO, (1,))
+        roots(0, "root0", HALVES[0:1])
+        roots(1, "root1", HALVES[0:1])
+        squares(0, "sq0", (1,))
+        squares(1, "sq1", (1,))
+        subtract(chunk(256, 1))
+        round_x(GS, 256, 256, 1, "xb1")
+        gather_table(0, 256, "diffB")
+        pick(chunk(512, 1)[0:1], "xb0")
+        response(0, DA)
+        roots(0, "root0", HALVES[1:2])
+        roots(1, "root1", HALVES[1:2])
+        factor(0, "w2raw00")
+        factor(1, "w2raw01")
+        quantize_x(256, 256, 1)
+        response(1, DB)
+        deviation(2, E, (0, 1), (0, 1))
+        product(0, m_tile("cmp0"))
+        deviation(3, OO, (0, 1), (0, 1))
+        spread_bias(0, "AA", DA)
+        turn_floats(0, "AA")
+        pick(chunk(512, 1)[1:4], "root0")
+        new_diff(512, 256, 1, "w2raw00")
+        subtract(chunk(512, 1))
+        round_x(GS, 512, 256, 1, "xb1")
+        squares(2, "sq0")
+        squares(3, "sq1")
+        roots(2, "root2")
+        empty(0, "AA", h_tile("hb0"))
+        product(1, m_tile("xb0"))
+        spread_bias(1, "AA", DB)
+        turn_floats(1, "AA")
+        gather_table(256, 256, "root0")
+        response(2, DA)
+        roots(3, "root1")
+        factor(2, "w2raw10")
+        quantize_x(512, 256, 1)
+        deviation(4, E, (0, 1), (0, 1))
+        deviation(5, OO, (0, 1), (0, 1))
+        quantize_h(0, "hq0")
+        pick(chunk(768, 1)[0:2], "w2raw00")
+        pick(chunk(768, 1)[2:4], "hb0")
+        empty(1, "AA", h_tile("sq1"))
+        response(3, DB)
+        quantize_h(1, "hq1")
+        factor(3, "w2raw11")
+        product(2, m_tile("cmp0"))
+        spread_bias(2, "AA", DA)
+        turn_floats(2, "AA")
+        squares(4, "sq0")
+        squares(5, "sq2")
+        new_diff(768, 256, 1, "root2")
+        subtract(chunk(768, 1))
+        round_x(GS, 768, 256, 1, "xb1")
+        scores(0, "o")
+        scores(1, "turn")
+        roots(4, "root1")
+        empty(2, "AA", h_tile("hb1"))
+        roots(5, "root3")
+        store(0, A, "res0")
+        store(1, A, "res1")
+        factor(4, "w2raw01")
+        gather_table(512, 256, "w2raw00")
+        product(3, m_tile("sq0"))
+        response(4, DA)
+        spread_bias(3, P3, DB)
+        turn_floats(3, P3)
+        quantize_x(768, 256, 1, sbuf([P, 256], U32, "w2raw11")[:])
+        deviation(6, E, (0, 1), (0, 1))
+        deviation(7, OO, (0, 1), (0, 1))
+        quantize_h(2, "hq2")
+        factor(5, "w2raw10")
+        squares(6, "sq1")
+        squares(7, "sq2")
+        product(4, m_tile("cmp0"))
+        spread_bias(4, P4, DA)
+        empty(3, P3, h_tile("hb2"))
+        turn_floats(4, P4)
+        response(5, DB)
+        gather_table(768, 256, "sq0")
+        response(6, E)
+        scores(2, "o")
+        roots(6, "root2")
+        roots(7, "root1", HALVES)
+        factor(6, "root3")
+        factor(7, "w2raw01", HALVES)
+        quantize_h(3, "hq0")
+        scores(3, "turn")
+        product(5, m_tile("xb0"))
+        spread_bias(5, P5, DB)
+        turn_floats(5, P5)
+        empty(4, P4, h_tile("hb1"))
+        response(7, DA)
+        store(2, A, "root2")
+        store(3, A, "res1")
+        product(6, m_tile("cmp0"))
+        quantize_h(4, "hq1")
+        scores(4, "o")
+        spread_bias(6, P6, E)
+        turn_floats(6, P6)
+        empty(5, P5, h_tile("hb2"))
+        spread_bias(7, "AV", DB)
+        product(7, m_tile("cmp1"))
+        quantize_h(5, "hq2")
+        turn_floats(7, "AV")
+        scores(5, "turn")
+        store(4, A, "res0")
+        empty(6, P6, h_tile("hb1"))
+        quantize_h(6, "hq0")
+        scores(6, "o")
+        empty(7, "AV", h_tile("hb2"))
+        quantize_h(7, "hq_last", True)
+        store(5, A, "res1")
+        last_scores(7, DA, ("xb0", "root0"))
+        store(6, A, "cmp0")

@@ -152,7 +152,10 @@ def tile_list_differential_star_photometry_kernel(
         def round_x(eng, lo, n, a, tag):
             tile, at = diff[lo, a]
             x_b[lo, a] = sbuf([P, n, 4], BF16, tag)
-            interleave(eng, x_b[lo, a][:], tile[:, :, at : at + n])
+            if lo and a:
+                eng(x_b[lo, a][:], tile[:, :, at : at + n].rearrange("p t c -> p c t"))
+            else:
+                interleave(eng, x_b[lo, a][:], tile[:, :, at : at + n])
 
         def quantize_x(lo, n, a, codes=None):
             codes, scales = quantize(

@@ -18,9 +18,9 @@ ACT = mybir.ActivationFunctionType
 ALU = mybir.AluOpType
 
 P = 128
+DIRECT = (4, 6, 7)
 WHOLE = (slice(0, 2),)
 HALVES = (slice(0, 1), slice(1, 2))
-PAIRS = ()
 
 
 def tile_list_differential_star_photometry_kernel(
@@ -51,11 +51,15 @@ def tile_list_differential_star_photometry_kernel(
         w3_s = sbuf([P, 2, N], U8, "w3_s")
         nc.vector.memset(tab_s[32:64, :].bitcast(I32), 0)
         nc.vector.memset(tab_s[64:128, :].bitcast(I32), 0)
+        w1_rows = sbuf([P, H], U8, "w1_rows")
+        nc.gpsimd.dma_start(w1_rows[0:32, :].bitcast(I32), w1_scales.rearrange("a q n -> (a q) n").bitcast(I32))
+        nc.vector.memset(w1_rows[32:64, :].bitcast(I32), 0)
+        nc.vector.memset(w1_rows[64:128, :].bitcast(I32), 0)
         ident = sbuf([P, P], F32, "ident")
         make_identity(nc, ident[:])
-        nc.gpsimd.memset(w1_s[:].bitcast(I32), 0)
-        nc.gpsimd.memset(v_s[:].bitcast(I32), 0)
-        nc.gpsimd.memset(w3_s[:].bitcast(I32), 0)
+        nc.vector.memset(w1_s[:].bitcast(I32), 0)
+        nc.vector.memset(v_s[:].bitcast(I32), 0)
+        nc.vector.memset(w3_s[:].bitcast(I32), 0)
         v_rows = sbuf([P, S], U8, "v_rows")
         nc.vector.tensor_copy(v_rows[:], tab_s[:].indirect(idx1[:]))
 
@@ -80,17 +84,18 @@ def tile_list_differential_star_photometry_kernel(
 
         def load_scales(plane, rows):
             for q in range(4):
-                nc.gpsimd.dma_start(
+                nc.sync.dma_start(
                     plane[32 * q : 32 * q + 4].bitcast(I32),
                     rows[:, 4 * q : 4 * q + 4, :].rearrange("a r n -> r a n").bitcast(I32),
                 )
 
-        def move_scales(a):
-            for q in range(4):
-                nc.gpsimd.dma_start(
-                    v_s[32 * q : 32 * q + 4, a, :].bitcast(I32),
-                    v_rows[16 * a + 4 * q : 16 * a + 4 * q + 4, :].bitcast(I32),
-                )
+        def move_scales(plane, rows):
+            for a in range(2):
+                for q in range(4):
+                    nc.gpsimd.dma_start(
+                        plane[32 * q : 32 * q + 4, a, :].bitcast(I32),
+                        rows[16 * a + 4 * q : 16 * a + 4 * q + 4, :].bitcast(I32),
+                    )
 
         A = nc.scalar.copy
         V = nc.vector.tensor_copy
@@ -113,7 +118,10 @@ def tile_list_differential_star_photometry_kernel(
 
         def round_w2(half, a, tag):
             w2_b[half, a] = sbuf([P, 512, 4], BF16, tag)
-            interleave(A, w2_b[half, a][:], w2_raw[half, a][:])
+            A(
+                w2_b[half, a][:].rearrange("p (s m) t -> p m t s", s=4),
+                w2_raw[half, a][:].rearrange("p t (m s) -> p m t s", s=4),
+            )
 
         def quantize_w2(half, a, codes=None):
             w2_q[half, a] = quantize(
@@ -171,23 +179,11 @@ def tile_list_differential_star_photometry_kernel(
                 for i in range(n // P):
                     v_w[lo // P + i, a] = words[:, a, P * i : P * (i + 1)]
 
-        def pairs_out(ap):
-            return ap.rearrange("j (u p e) -> j u p e", u=2, e=2)
+        def by_entry(ap):
+            return ap.rearrange("p (s j) -> p j s", s=4)
 
-        def pairs_in(ap):
-            return ap.rearrange("j (p u e) -> j u p e", u=2, e=2)
-
-        def quads_out(ap):
-            return ap.rearrange("j (t c i) -> j c t i", t=4, i=4)
-
-        def quads_in(ap):
-            return ap.rearrange("j (c i t) -> j c t i", t=4, i=4)
-
-        def walk_out(jt, ap):
-            return pairs_out(ap) if jt in PAIRS else quads_out(ap)
-
-        def walk_in(jt, ap):
-            return pairs_in(ap) if jt in PAIRS else quads_in(ap)
+        def in_words(ap):
+            return ap.rearrange("p (j s) -> p j s", s=4)
 
         damp = {}
 
@@ -216,7 +212,10 @@ def tile_list_differential_star_photometry_kernel(
             if 0 in halves:
                 square[jt] = sbuf([P, 2, 512], F32, tag)
             for half in halves:
-                nc.scalar.activation(walk_out(jt, square[jt][:, half, :]), walk_in(jt, e_bank[jt, half][:]), ACT.Square)
+                if jt in DIRECT:
+                    nc.scalar.activation(in_words(square[jt][:, half, :]), by_entry(e_bank[jt, half][:]), ACT.Square)
+                else:
+                    nc.scalar.activation(square[jt][:, half, :], e_bank[jt, half][:], ACT.Square)
 
         def roots(jt, tag, parts=WHOLE):
             if parts[0].start == 0:
@@ -230,6 +229,10 @@ def tile_list_differential_star_photometry_kernel(
             for part in parts:
                 nc.scalar.activation(damp[jt][:, part], root[jt][:, part], ACT.Square)
 
+        def factor_on_gpsimd(jt, tag):
+            damp[jt] = sbuf([P, 2, 512], F32, tag)
+            nc.gpsimd.tensor_tensor(damp[jt][:], root[jt][:], root[jt][:], ALU.mult)
+
         damped = {}
 
         def response(jt, banks):
@@ -241,36 +244,66 @@ def tile_list_differential_star_photometry_kernel(
                         d[:],
                         lhsT=v_w[jt, a].bitcast(FP8X4),
                         lhsT_scale=v_s[:, a, jt * P : (jt + 1) * P],
-                        rhs=w1_w[:, a, 1024 * half : 1024 * (half + 1)].bitcast(FP4X4),
+                        rhs=w1_d[:, a, 1024 * half : 1024 * (half + 1)].bitcast(FP4X4),
                         rhs_scale=w1_s[:, a, 512 * half : 512 * (half + 1)],
                         start=(a == 0),
                         stop=(a == 1),
                     )
 
-        def product(jt, tile):
+        def product(jt, tile, halves=(0, 1)):
             damped[jt] = tile
-            for half in range(2):
-                nc.vector.tensor_tensor(
-                    walk_out(jt, damped[jt][:, half, :]), walk_in(jt, d_bank[jt, half][:]),
-                    walk_out(jt, damp[jt][:, half, :]), ALU.mult,
-                )
+            for half in halves:
+                if jt in DIRECT:
+                    nc.vector.tensor_tensor(
+                        in_words(tile[:, half, :]), by_entry(d_bank[jt, half][:]), in_words(damp[jt][:, half, :]),
+                        ALU.mult,
+                    )
+                else:
+                    nc.vector.tensor_tensor(tile[:, half, :], d_bank[jt, half][:], damp[jt][:, half, :], ALU.mult)
 
-        h_rows = {}
+        def direct_deviation(jt, banks):
+            for half in range(2):
+                e_bank[jt, half] = bank(banks[half])
+                for s in range(4):
+                    for a in range(2):
+                        nc.tensor.matmul_mx(
+                            e_bank[jt, half][:, P * s : P * (s + 1)],
+                            lhsT=w2_q[half, a][0][:, P * s : P * (s + 1)].bitcast(FP8X4),
+                            lhsT_scale=w2_q[half, a][1][:, P * s : P * (s + 1)],
+                            rhs=x_q[jt, a][0].bitcast(FP8X4),
+                            rhs_scale=x_q[jt, a][1],
+                            start=(a == 0),
+                            stop=(a == 1),
+                        )
+
+        def direct_response(jt, banks):
+            for half in range(2):
+                d_bank[jt, half] = bank(banks[half])
+                for s in range(4):
+                    at = 512 * half + P * s
+                    for a in range(2):
+                        nc.tensor.matmul_mx(
+                            d_bank[jt, half][:, P * s : P * (s + 1)],
+                            lhsT=w1_d[:, a, 2 * at : 2 * (at + P)].bitcast(FP4X4),
+                            lhsT_scale=w1_s[:, a, at : at + P],
+                            rhs=v_w[jt, a].bitcast(FP8X4),
+                            rhs_scale=v_s[:, a, jt * P : (jt + 1) * P],
+                            start=(a == 0),
+                            stop=(a == 1),
+                        )
+
+        def add_bias(jt, tile, halves=(0, 1)):
+            h_b[jt] = tile
+            part = slice(halves[0], halves[-1] + 1)
+            nc.vector.tensor_tensor(
+                tile[:, part].rearrange("p a j t -> p (a j t)"), damped[jt][:, part].rearrange("p a c -> p (a c)"),
+                b_rep[:, part].rearrange("p a j t -> p (a j t)"), ALU.add,
+            )
+
         h_b = {}
         h_q = {}
 
         turned = {}
-
-        def turn(jt, banks):
-            words = h_rows[jt][:].bitcast(F32)
-            per = 2 // len(banks)
-            turned[jt] = [bank(name) for name in banks]
-            for half in range(2):
-                for u in range(2):
-                    i = 2 * (half % per) + u
-                    nc.tensor.transpose(
-                        turned[jt][half // per][:, P * i : P * (i + 1)], words[:, half, P * u : P * (u + 1)], ident[:]
-                    )
 
         def spread_bias(jt, engines, banks):
             turned[jt] = [bank(name) for name in banks]
@@ -336,6 +369,12 @@ def tile_list_differential_star_photometry_kernel(
             eng(result[:].rearrange("p n j -> p (n j)"), o_bank[jt][:])
             nc.sync.dma_start(out[:, jt * P : (jt + 1) * P].rearrange("(n p) j -> p n j", p=P), result[:])
 
+        def store_pair(jt, tag):
+            result = sbuf([P, 4, 2 * P], F32, tag)
+            for i in range(2):
+                A(result[:, :, P * i : P * (i + 1)], o_bank[jt + i][:].rearrange("p (n j) -> p n j", n=4))
+            nc.sync.dma_start(out[:, jt * P : (jt + 2) * P].rearrange("(n p) j -> p n j", p=P), result[:])
+
         def last_scores(jt, banks, tags):
             accs = [bank(name) for name in banks]
             for a in range(2):
@@ -357,7 +396,6 @@ def tile_list_differential_star_photometry_kernel(
                     result[:],
                 )
 
-        G = nc.gpsimd
         DA = ("d0", "d1")
         DB = ("d2", "d3")
         E = ("e0", "e1")
@@ -373,13 +411,18 @@ def tile_list_differential_star_photometry_kernel(
         load_w2(0, 0)
         load_w2(0, 1)
         load_w2(1, 0)
+        w1_w = sbuf([P, 2, 2 * H], U8, "w1_w")
+        nc.sync.dma_start(w1_w[:].bitcast(I32), w1_words.rearrange("a p n -> p a n").bitcast(I32))
         for t in range(4):
             load_plane(1, t)
         load_w2(1, 1)
-        load_scales(w1_s, w1_scales)
-        move_scales(0)
-        move_scales(1)
-        load_scales(w3_s, w3_scales)
+        w1_dealt_rows = sbuf([P, H], U8, "w1_dealt_rows")
+        nc.gpsimd.tensor_copy(
+            w1_dealt_rows[:].rearrange("p (g s m) -> p g s m", g=2, s=4),
+            w1_rows[:].rearrange("p (g m s) -> p g s m", g=2, s=4),
+        )
+        move_scales(v_s, v_rows)
+        move_scales(w1_s, w1_dealt_rows)
 
         b_quads = sbuf([P, 2, 512], F32, "b_quads")
         for a in range(2):
@@ -405,15 +448,19 @@ def tile_list_differential_star_photometry_kernel(
             subtract(units)
         load_table(0, "plane00")
         load_table(1, "plane01")
-        w1_w = sbuf([P, 2, 2 * H], U8, "w1_w")
-        nc.sync.dma_start(w1_w[:].bitcast(I32), w1_words.rearrange("a p n -> p a n").bitcast(I32))
         w3_w = sbuf([P, 2, N], U32, "w3_w")
         nc.sync.dma_start(w3_w[:].bitcast(I32), w3_words.rearrange("a p n i -> p a (n i)").bitcast(I32))
+        load_scales(w3_s, w3_scales)
         round_w2(0, 0, "w2b0")
         quantize_w2(0, 0)
         round_w2(0, 1, "w2b1")
         quantize_w2(0, 1)
         round_w2(1, 0, "w2b2")
+        w1_d = sbuf([P, 2, 2 * H], U8, "w1_d")
+        A(
+            w1_d[:].bitcast(U16).rearrange("p a (g s m) -> p (a g) s m", g=2, s=4),
+            w1_w[:].bitcast(U16).rearrange("p a (g m s) -> p (a g) s m", g=2, s=4),
+        )
         round_x(A, 0, 512, 0, "w2raw01")
         round_x(A, 512, 512, 0, "w2raw10")
         new_diff(0, 256, 1, "diffB")
@@ -474,7 +521,7 @@ def tile_list_differential_star_photometry_kernel(
         roots(3, "root1")
         factor(2, "w2raw10")
         quantize_x(512, 256, 1)
-        deviation(4, E, (0, 1), (0, 1))
+        direct_deviation(4, E)
         deviation(5, OO, (0, 1), (0, 1))
         quantize_h(0, "hq0")
         pick(chunk(768, 1)[0:2], "w2raw00")
@@ -496,59 +543,55 @@ def tile_list_differential_star_photometry_kernel(
         roots(4, "root1")
         empty(2, "AA", h_tile("hb1"))
         roots(5, "root3")
-        store(0, A, "res0")
-        store(1, A, "res1")
+        store_pair(0, "res0")
         factor(4, "w2raw01")
         gather_table(512, 256, "w2raw00")
         product(3, m_tile("sq0"))
-        response(4, DA)
-        spread_bias(3, P3, DB)
-        turn_floats(3, P3)
+        direct_response(4, DA)
+        spread_bias(3, "VV", DB)
+        turn_floats(3, "VV")
         quantize_x(768, 256, 1, sbuf([P, 256], U32, "w2raw11")[:])
-        deviation(6, E, (0, 1), (0, 1))
-        deviation(7, OO, (0, 1), (0, 1))
+        direct_deviation(6, E)
+        direct_deviation(7, OO)
         quantize_h(2, "hq2")
         factor(5, "w2raw10")
         squares(6, "sq1")
-        squares(7, "sq2")
+        squares(7, "sq2", (0,))
+        roots(6, "root2")
+        squares(7, "sq2", (1,))
+        factor(6, "root3")
         product(4, m_tile("cmp0"))
-        spread_bias(4, P4, DA)
-        empty(3, P3, h_tile("hb2"))
-        turn_floats(4, P4)
+        empty(3, "VV", h_tile("hb2"))
         response(5, DB)
         gather_table(768, 256, "sq0")
-        response(6, E)
-        scores(2, "o")
-        roots(6, "root2")
-        roots(7, "root1", HALVES)
-        factor(6, "root3")
-        factor(7, "w2raw01", HALVES)
+        scores(2, "d0")
+        direct_response(6, E)
         quantize_h(3, "hq0")
-        scores(3, "turn")
+        scores(3, "d1")
         product(5, m_tile("xb0"))
-        spread_bias(5, P5, DB)
-        turn_floats(5, P5)
-        empty(4, P4, h_tile("hb1"))
-        response(7, DA)
-        store(2, A, "root2")
-        store(3, A, "res1")
+        spread_bias(5, "AA", DB)
+        turn_floats(5, "AA")
+        direct_response(7, OO)
+        add_bias(4, h_tile("hb1"))
+        roots(7, "root1", HALVES)
+        store_pair(2, "res0")
+        factor(7, "w2raw01", HALVES)
         product(6, m_tile("cmp0"))
         quantize_h(4, "hq1")
-        scores(4, "o")
-        spread_bias(6, P6, E)
-        turn_floats(6, P6)
-        empty(5, P5, h_tile("hb2"))
-        spread_bias(7, "AV", DB)
-        product(7, m_tile("cmp1"))
-        quantize_h(5, "hq2")
-        turn_floats(7, "AV")
-        scores(5, "turn")
-        store(4, A, "res0")
-        empty(6, P6, h_tile("hb1"))
+        scores(4, "e0")
+        empty(5, "AA", h_tile("hb2"))
+        add_bias(6, h_tile("hb1"))
+        last = m_tile("cmp1")
+        product(7, last)
         quantize_h(6, "hq0")
-        scores(6, "o")
-        empty(7, "AV", h_tile("hb2"))
+        scores(6, "e1")
+        store(4, A, "root2")
+        last_h = h_tile("hb0")
+        add_bias(7, last_h, (0,))
+        quantize_h(5, "hq2")
+        scores(5, "d0")
+        add_bias(7, last_h, (1,))
         quantize_h(7, "hq_last", True)
-        store(5, A, "res1")
-        last_scores(7, DA, ("xb0", "root0"))
-        store(6, A, "cmp0")
+        store(6, A, "sq2")
+        store(5, A, "sq1")
+        last_scores(7, OO, ("xb0", "root0"))

@@ -264,16 +264,16 @@ def tile_list_differential_star_photometry_kernel(
         def direct_deviation(jt, banks):
             for half in range(2):
                 e_bank[jt, half] = bank(banks[half])
-                for s in range(4):
-                    for a in range(2):
+                for a in range(2):
+                    for s in range(4):
                         nc.tensor.matmul_mx(
                             e_bank[jt, half][:, P * s : P * (s + 1)],
                             lhsT=w2_q[half, a][0][:, P * s : P * (s + 1)].bitcast(FP8X4),
                             lhsT_scale=w2_q[half, a][1][:, P * s : P * (s + 1)],
                             rhs=x_q[jt, a][0].bitcast(FP8X4),
                             rhs_scale=x_q[jt, a][1],
-                            start=(a == 0),
-                            stop=(a == 1),
+                            start=(a == 0 and s == 0),
+                            stop=(a == 1 and s == 3),
                         )
 
         def direct_response(jt, banks):
@@ -292,10 +292,10 @@ def tile_list_differential_star_photometry_kernel(
                             stop=(a == 1),
                         )
 
-        def add_bias(jt, tile, halves=(0, 1)):
+        def add_bias(jt, tile, halves=(0, 1), eng=nc.vector):
             h_b[jt] = tile
             part = slice(halves[0], halves[-1] + 1)
-            nc.vector.tensor_tensor(
+            eng.tensor_tensor(
                 tile[:, part].rearrange("p a j t -> p (a j t)"), damped[jt][:, part].rearrange("p a c -> p (a c)"),
                 b_rep[:, part].rearrange("p a j t -> p (a j t)"), ALU.add,
             )
@@ -338,14 +338,24 @@ def tile_list_differential_star_photometry_kernel(
         def h_tile(tag):
             return sbuf([P, 2, P, 4], BF16, tag)[:]
 
-        def quantize_h(jt, tag, split=False):
+        def quantize_h(jt, tag, split=False, codes=None):
             if split:
                 for a in range(2):
                     h_q[jt, a] = quantize(h_b[jt][:, a].rearrange("p j t -> p (j t)"), P, "%s%d" % (tag, a))
             else:
-                codes, scales = quantize(h_b[jt].rearrange("p a j t -> p (a j t)"), 2 * P, tag)
+                into = sbuf([P, 2 * P], U32, codes)[:] if codes else None
+                codes, scales = quantize(h_b[jt].rearrange("p a j t -> p (a j t)"), 2 * P, tag, into)
                 for a in range(2):
                     h_q[jt, a] = (codes[:, P * a : P * (a + 1)], scales[:, P * a : P * (a + 1)])
+
+        def add_bias_half(jt, half, tag, eng):
+            h_b[jt, half] = sbuf([P, 512], BF16, tag)
+            eng.tensor_tensor(
+                h_b[jt, half][:], damped[jt][:, half], b_rep[:, half].rearrange("p j t -> p (j t)"), ALU.add
+            )
+
+        def quantize_half(jt, half, tag, codes):
+            h_q[jt, half] = quantize(h_b[jt, half][:], P, tag, sbuf([P, P], U32, codes)[:])
 
         o_bank = {}
 
@@ -492,7 +502,7 @@ def tile_list_differential_star_photometry_kernel(
         subtract(chunk(256, 1))
         round_x(GS, 256, 256, 1, "xb1")
         gather_table(0, 256, "diffB")
-        pick(chunk(512, 1)[0:1], "xb0")
+        pick(chunk(512, 1)[0:2], "xb0")
         response(0, DA)
         roots(0, "root0", HALVES[1:2])
         roots(1, "root1", HALVES[1:2])
@@ -505,7 +515,7 @@ def tile_list_differential_star_photometry_kernel(
         deviation(3, OO, (0, 1), (0, 1))
         spread_bias(0, "AA", DA)
         turn_floats(0, "AA")
-        pick(chunk(512, 1)[1:4], "root0")
+        pick(chunk(512, 1)[2:4], "root0")
         new_diff(512, 256, 1, "w2raw00")
         subtract(chunk(512, 1))
         round_x(GS, 512, 256, 1, "xb1")
@@ -554,44 +564,45 @@ def tile_list_differential_star_photometry_kernel(
         direct_deviation(6, E)
         direct_deviation(7, OO)
         quantize_h(2, "hq2")
-        factor(5, "w2raw10")
+        factor_on_gpsimd(5, "xb1")
         squares(6, "sq1")
-        squares(7, "sq2", (0,))
-        roots(6, "root2")
-        squares(7, "sq2", (1,))
-        factor(6, "root3")
-        product(4, m_tile("cmp0"))
+        roots(6, "root2", HALVES)
+        factor(6, "root3", HALVES)
+        squares(7, "sq2")
+        gather_table(768, 256, "hb1")
         empty(3, "VV", h_tile("hb2"))
         response(5, DB)
-        gather_table(768, 256, "sq0")
-        scores(2, "d0")
         direct_response(6, E)
         quantize_h(3, "hq0")
+        product(4, m_tile("cmp0"))
+        scores(2, "d0")
         scores(3, "d1")
+        add_bias_half(4, 0, "hb2", nc.gpsimd)
         product(5, m_tile("xb0"))
         spread_bias(5, "AA", DB)
         turn_floats(5, "AA")
         direct_response(7, OO)
-        add_bias(4, h_tile("hb1"))
         roots(7, "root1", HALVES)
         store_pair(2, "res0")
         factor(7, "w2raw01", HALVES)
-        product(6, m_tile("cmp0"))
-        quantize_h(4, "hq1")
+        product(6, m_tile("w2raw00"))
+        add_bias_half(4, 1, "root3", nc.vector)
+        add_bias(6, h_tile("sq0"))
+        quantize_half(4, 0, "hq1a", "cmp0")
+        quantize_half(4, 1, "hq1b", "hq1")
         scores(4, "e0")
-        empty(5, "AA", h_tile("hb2"))
-        add_bias(6, h_tile("hb1"))
-        last = m_tile("cmp1")
-        product(7, last)
+        empty(5, "AA", h_tile("w2raw10"))
         quantize_h(6, "hq0")
         scores(6, "e1")
+        last = m_tile("cmp1")
+        product(7, last)
         store(4, A, "root2")
+        store(6, A, "sq2")
         last_h = h_tile("hb0")
-        add_bias(7, last_h, (0,))
         quantize_h(5, "hq2")
         scores(5, "d0")
+        add_bias(7, last_h, (0,))
         add_bias(7, last_h, (1,))
         quantize_h(7, "hq_last", True)
-        store(6, A, "sq2")
         store(5, A, "sq1")
         last_scores(7, OO, ("xb0", "root0"))

@@ -474,10 +474,11 @@ def tile_list_differential_star_photometry_kernel(
         round_x(A, 0, 512, 0, "w2raw01")
         round_x(A, 512, 512, 0, "w2raw10")
         new_diff(0, 256, 1, "diffB")
-        pick(chunk(0, 1)[0:2], "cmp0")
-        subtract(chunk(0, 1)[0:2])
-        pick(chunk(0, 1)[2:4], "plane02")
-        subtract(chunk(0, 1)[2:4])
+        for t in range(4):
+            units = [(0, P, 1, t), (P, P, 1, t)]
+            pick(units[0:1], ("cmp0", "xb1", "cmp0", "plane02")[t])
+            pick(units[1:2], ("cmp1", "xb0", "cmp1", "root0")[t])
+            subtract(units)
         round_x(A, 0, 256, 1, "xb0")
         round_w2(1, 1, "w2b3")
         late = sbuf([P, 3, 512], U32, "plane02")
@@ -535,7 +536,7 @@ def tile_list_differential_star_photometry_kernel(
         deviation(5, OO, (0, 1), (0, 1))
         quantize_h(0, "hq0")
         pick(chunk(768, 1)[0:2], "w2raw00")
-        pick(chunk(768, 1)[2:4], "hb0")
+        pick(chunk(768, 1)[2:4], "xb1")
         empty(1, "AA", h_tile("sq1"))
         response(3, DB)
         quantize_h(1, "hq1")
@@ -547,7 +548,7 @@ def tile_list_differential_star_photometry_kernel(
         squares(5, "sq2")
         new_diff(768, 256, 1, "root2")
         subtract(chunk(768, 1))
-        round_x(GS, 768, 256, 1, "xb1")
+        round_x(GS, 768, 256, 1, "hb0")
         scores(0, "o")
         scores(1, "turn")
         roots(4, "root1")
@@ -564,7 +565,7 @@ def tile_list_differential_star_photometry_kernel(
         direct_deviation(6, E)
         direct_deviation(7, OO)
         quantize_h(2, "hq2")
-        factor_on_gpsimd(5, "xb1")
+        factor_on_gpsimd(5, "hb0")
         squares(6, "sq1")
         roots(6, "root2", HALVES)
         factor(6, "root3", HALVES)
@@ -573,8 +574,8 @@ def tile_list_differential_star_photometry_kernel(
         empty(3, "VV", h_tile("hb2"))
         response(5, DB)
         direct_response(6, E)
-        quantize_h(3, "hq0")
         product(4, m_tile("cmp0"))
+        quantize_h(3, "hq0", codes="w2raw01")
         scores(2, "d0")
         scores(3, "d1")
         add_bias_half(4, 0, "hb2", nc.gpsimd)
@@ -598,7 +599,7 @@ def tile_list_differential_star_photometry_kernel(
         product(7, last)
         store(4, A, "root2")
         store(6, A, "sq2")
-        last_h = h_tile("hb0")
+        last_h = h_tile("xb1")
         quantize_h(5, "hq2")
         scores(5, "d0")
         add_bias(7, last_h, (0,))

@@ -446,6 +446,8 @@ def tile_list_differential_star_photometry_kernel(
         for a in range(2):
             nc.scalar.copy(b_rep[:, a], b_col[:, a : a + 1, :].to_broadcast([P, P, 4]))
 
+        warm = sbuf([P, 8], F32, "warm")
+        nc.scalar.activation(warm[:], b_col[:].rearrange("p a t -> p (a t)"), ACT.Abs_reciprocal_sqrt, bias=1.0)
         OO = ("turn", "o")
         P3 = "VV"
         P4 = "VV"

from contextlib import ExitStack

import concourse.mybir as mybir
from concourse.masks import make_identity

K, H, N, T, S = 1024, 1024, 512, 2048, 1024
FLOPS = 2 * S * (K * H + K * H + H * N)

F32 = mybir.dt.float32
BF16 = mybir.dt.bfloat16
I32 = mybir.dt.int32
U32 = mybir.dt.uint32
U16 = mybir.dt.uint16
U8 = mybir.dt.uint8
FP8X4 = mybir.dt.float8_e4m3fn_x4
FP4X4 = mybir.dt.float4_e2m1fn_x4
ACT = mybir.ActivationFunctionType
ALU = mybir.AluOpType

P = 128
DIRECT = (4, 6, 7)
WHOLE = (slice(0, 2),)
HALVES = (slice(0, 1), slice(1, 2))


def tile_list_differential_star_photometry_kernel(
    tc, tab_words, tab_scales, offs, xT, offs2, offs3, w1_words, w1_scales, w2, b, w3_words, w3_scales, out
):
    nc = tc.nc
    with ExitStack() as ctx:
        lists = ctx.enter_context(tc.tile_pool(name="lists", bufs=1))
        sb = ctx.enter_context(tc.tile_pool(name="sb", bufs=1))
        ps = ctx.enter_context(tc.psum_pool(name="ps", bufs=1))

        def sbuf(shape, dtype, tag):
            return sb.tile(shape, dtype, name=tag, tag=tag, align_bytes=64)

        def bank(tag):
            return ps.tile([P, 512], F32, name=tag, tag=tag)

        idx1 = lists.tile([P, S // 16], U16, name="idx1")
        idx2 = lists.tile([P, S // 16], U16, name="idx2")
        idx3 = lists.tile([P, S // 16], U16, name="idx3")
        tab_s = sbuf([P, T], U8, "tab_s")
        nc.sync.dma_start(idx1[:], offs)
        nc.sync.dma_start(tab_s[0:32, :].bitcast(I32), tab_scales.rearrange("a q n -> (a q) n").bitcast(I32))
        nc.sync.dma_start(idx3[:], offs3)
        nc.sync.dma_start(idx2[:], offs2)
        w1_s = sbuf([P, 2, H], U8, "w1_s")
        v_s = sbuf([P, 2, S], U8, "v_s")
        w3_s = sbuf([P, 2, N], U8, "w3_s")
        nc.vector.memset(tab_s[32:64, :].bitcast(I32), 0)
        nc.vector.memset(tab_s[64:128, :].bitcast(I32), 0)
        w1_rows = sbuf([P, H], U8, "w1_rows")
        nc.gpsimd.dma_start(w1_rows[0:32, :].bitcast(I32), w1_scales.rearrange("a q n -> (a q) n").bitcast(I32))
        nc.vector.memset(w1_rows[32:64, :].bitcast(I32), 0)
        nc.vector.memset(w1_rows[64:128, :].bitcast(I32), 0)
        ident = sbuf([P, P], F32, "ident")
        make_identity(nc, ident[:])
        nc.vector.memset(w1_s[:].bitcast(I32), 0)
        nc.vector.memset(v_s[:].bitcast(I32), 0)
        nc.vector.memset(w3_s[:].bitcast(I32), 0)
        v_rows = sbuf([P, S], U8, "v_rows")
        nc.vector.tensor_copy(v_rows[:], tab_s[:].indirect(idx1[:]))

        planes = {}
        w2_raw = {}
        tab_w = {}

        def load_plane(a, t):
            planes[a, t] = sbuf([P, T], F32, "plane%d%d" % (a, t))
            nc.sync.dma_start(planes[a, t][:], xT[512 * a + t : 512 * (a + 1) : 4, :])

        def load_w2(half, a):
            w2_raw[half, a] = sbuf([P, 4, 512], F32, "w2raw%d%d" % (half, a))
            nc.sync.dma_start(
                w2_raw[half, a][:],
                w2[512 * a : 512 * (a + 1), 512 * half : 512 * (half + 1)].rearrange("(p t) c -> p t c", t=4),
            )

        def load_table(a, tag):
            tab_w[a] = sbuf([P, T], U32, tag)
            nc.sync.dma_start(tab_w[a][:].bitcast(I32), tab_words[a].rearrange("p n i -> p (n i)").bitcast(I32))

        def load_scales(plane, rows):
            for q in range(4):
                nc.sync.dma_start(
                    plane[32 * q : 32 * q + 4].bitcast(I32),
                    rows[:, 4 * q : 4 * q + 4, :].rearrange("a r n -> r a n").bitcast(I32),
                )

        def move_scales(plane, rows):
            for a in range(2):
                for q in range(4):
                    nc.gpsimd.dma_start(
                        plane[32 * q : 32 * q + 4, a, :].bitcast(I32),
                        rows[16 * a + 4 * q : 16 * a + 4 * q + 4, :].bitcast(I32),
                    )

        A = nc.scalar.copy
        V = nc.vector.tensor_copy

        def GS(dst, src):
            nc.gpsimd.tensor_scalar(dst, src, 1.0, 0.0, ALU.mult, ALU.add)

        def interleave(eng, dst, src):
            eng(dst.rearrange("p (c i) t -> p c t i", i=4), src.rearrange("p t (c i) -> p c t i", i=4))

        def quantize(src, width, tag, codes=None):
            if codes is None:
                codes = sbuf([P, width], U32, tag + "_c")[:]
            scales = sbuf([P, width], U8, tag + "_s")
            nc.vector.quantize_mx(out=codes.bitcast(FP8X4), scales=scales[:], in_=src)
            return codes, scales[:]

        w2_b = {}
        w2_q = {}

        def round_w2(half, a, tag):
            w2_b[half, a] = sbuf([P, 512, 4], BF16, tag)
            A(
                w2_b[half, a][:].rearrange("p (s m) t -> p m t s", s=4),
                w2_raw[half, a][:].rearrange("p t (m s) -> p m t s", s=4),
            )

        def quantize_w2(half, a, codes=None):
            w2_q[half, a] = quantize(
                w2_b[half, a][:].rearrange("p c t -> p (c t)"), 512, "w2q%d%d" % (half, a), codes
            )

        diff = {}
        other = {}
        x_b = {}
        x_q = {}
        v_w = {}

        def new_diff(lo, n, a, tag):
            tile = sbuf([P, 4, n], F32, tag)
            for at in range(0, n, P):
                diff[lo + at, a] = (tile, at)

        def pick(units, tag):
            tile = sbuf([P, sum(u[1] for u in units)], F32, tag)
            at = 0
            for lo, n, a, t in units:
                other[lo, n, a, t] = tile[:, at : at + n]
                nc.vector.tensor_copy(
                    other[lo, n, a, t], planes[a, t][:].indirect(idx3[:, lo // 16 : (lo + n) // 16])
                )
                at = at + n

        def subtract(units):
            for lo, n, a, t in units:
                tile, at = diff[lo, a]
                nc.vector.tensor_tensor(
                    tile[:, t, at : at + n], planes[a, t][:].indirect(idx2[:, lo // 16 : (lo + n) // 16]),
                    other[lo, n, a, t], ALU.subtract,
                )

        def round_x(eng, lo, n, a, tag):
            tile, at = diff[lo, a]
            x_b[lo, a] = sbuf([P, n, 4], BF16, tag)
            if lo and a:
                eng(x_b[lo, a][:], tile[:, :, at : at + n].rearrange("p t c -> p c t"))
            else:
                interleave(eng, x_b[lo, a][:], tile[:, :, at : at + n])

        def quantize_x(lo, n, a, codes=None):
            codes, scales = quantize(
                x_b[lo, a][:].rearrange("p c t -> p (c t)"), n, "xq%d_%d" % (lo, a), codes
            )
            for i in range(n // P):
                x_q[lo // P + i, a] = (codes[:, P * i : P * (i + 1)], scales[:, P * i : P * (i + 1)])

        def gather_table(lo, n, tag):
            words = sbuf([P, 2, n], U32, tag)
            for a in range(2):
                nc.vector.tensor_copy(words[:, a, :], tab_w[a][:].indirect(idx1[:, lo // 16 : (lo + n) // 16]))
                for i in range(n // P):
                    v_w[lo // P + i, a] = words[:, a, P * i : P * (i + 1)]

        def by_entry(ap):
            return ap.rearrange("p (s j) -> p j s", s=4)

        def in_words(ap):
            return ap.rearrange("p (j s) -> p j s", s=4)

        damp = {}

        square = {}
        root = {}

        e_bank = {}
        d_bank = {}

        def deviation(jt, banks, halves=(0, 1), passes=(1, 0)):
            for half in halves:
                e = bank(banks[half])
                e_bank[jt, half] = e
                for a in passes:
                    nc.tensor.matmul_mx(
                        e[:],
                        lhsT=x_q[jt, a][0].bitcast(FP8X4),
                        lhsT_scale=x_q[jt, a][1],
                        rhs=w2_q[half, a][0].bitcast(FP8X4),
                        rhs_scale=w2_q[half, a][1],
                        start=(a == passes[0]),
                        stop=(a == passes[1]),
                    )

        def squares(jt, tag, halves=(0, 1)):
            if 0 in halves:
                square[jt] = sbuf([P, 2, 512], F32, tag)
            for half in halves:
                if jt in DIRECT:
                    nc.scalar.activation(in_words(square[jt][:, half, :]), by_entry(e_bank[jt, half][:]), ACT.Square)
                else:
                    nc.scalar.activation(square[jt][:, half, :], e_bank[jt, half][:], ACT.Square)

        def roots(jt, tag, parts=WHOLE):
            if parts[0].start == 0:
                root[jt] = sbuf([P, 2, 512], F32, tag)
            for part in parts:
                nc.scalar.activation(root[jt][:, part], square[jt][:, part], ACT.Abs_reciprocal_sqrt, bias=1.0)

        def factor(jt, tag, parts=WHOLE):
            if parts[0].start == 0:
                damp[jt] = sbuf([P, 2, 512], F32, tag)
            for part in parts:
                nc.scalar.activation(damp[jt][:, part], root[jt][:, part], ACT.Square)

        def factor_on_gpsimd(jt, tag):
            damp[jt] = sbuf([P, 2, 512], F32, tag)
            nc.gpsimd.tensor_tensor(damp[jt][:], root[jt][:], root[jt][:], ALU.mult)

        damped = {}

        def response(jt, banks):
            for half in range(2):
                d = bank(banks[half])
                d_bank[jt, half] = d
                for a in range(2):
                    nc.tensor.matmul_mx(
                        d[:],
                        lhsT=v_w[jt, a].bitcast(FP8X4),
                        lhsT_scale=v_s[:, a, jt * P : (jt + 1) * P],
                        rhs=w1_d[:, a, 1024 * half : 1024 * (half + 1)].bitcast(FP4X4),
                        rhs_scale=w1_s[:, a, 512 * half : 512 * (half + 1)],
                        start=(a == 0),
                        stop=(a == 1),
                    )

        def product(jt, tile, halves=(0, 1)):
            damped[jt] = tile
            for half in halves:
                if jt in DIRECT:
                    nc.vector.tensor_tensor(
                        in_words(tile[:, half, :]), by_entry(d_bank[jt, half][:]), in_words(damp[jt][:, half, :]),
                        ALU.mult,
                    )
                else:
                    nc.vector.tensor_tensor(tile[:, half, :], d_bank[jt, half][:], damp[jt][:, half, :], ALU.mult)

        def direct_deviation(jt, banks):
            for half in range(2):
                e_bank[jt, half] = bank(banks[half])
                for a in range(2):
                    for s in range(4):
                        nc.tensor.matmul_mx(
                            e_bank[jt, half][:, P * s : P * (s + 1)],
                            lhsT=w2_q[half, a][0][:, P * s : P * (s + 1)].bitcast(FP8X4),
                            lhsT_scale=w2_q[half, a][1][:, P * s : P * (s + 1)],
                            rhs=x_q[jt, a][0].bitcast(FP8X4),
                            rhs_scale=x_q[jt, a][1],
                            start=(a == 0 and s == 0),
                            stop=(a == 1 and s == 3),
                        )

        def direct_response(jt, banks):
            for half in range(2):
                d_bank[jt, half] = bank(banks[half])
                for s in range(4):
                    at = 512 * half + P * s
                    for a in range(2):
                        nc.tensor.matmul_mx(
                            d_bank[jt, half][:, P * s : P * (s + 1)],
                            lhsT=w1_d[:, a, 2 * at : 2 * (at + P)].bitcast(FP4X4),
                            lhsT_scale=w1_s[:, a, at : at + P],
                            rhs=v_w[jt, a].bitcast(FP8X4),
                            rhs_scale=v_s[:, a, jt * P : (jt + 1) * P],
                            start=(a == 0),
                            stop=(a == 1),
                        )

        def add_bias(jt, tile, halves=(0, 1), eng=nc.vector):
            h_b[jt] = tile
            part = slice(halves[0], halves[-1] + 1)
            eng.tensor_tensor(
                tile[:, part].rearrange("p a j t -> p (a j t)"), damped[jt][:, part].rearrange("p a c -> p (a c)"),
                b_rep[:, part].rearrange("p a j t -> p (a j t)"), ALU.add,
            )

        h_b = {}
        h_q = {}

        turned = {}

        def spread_bias(jt, engines, banks):
            turned[jt] = [bank(name) for name in banks]
            for half in range(2):
                if engines[half] == "A":
                    for t in range(4):
                        nc.tensor.matmul(
                            turned[jt][half][:, P * t : P * (t + 1)], b_quads[:, half, P * t : P * (t + 1)], ident[:],
                            start=(t == 0), stop=False, is_transpose=True,
                        )

        def turn_floats(jt, engines):
            for half in range(2):
                for t in range(4):
                    nc.tensor.matmul(
                        turned[jt][half][:, P * t : P * (t + 1)], damped[jt][:, half, P * t : P * (t + 1)], ident[:],
                        start=(t == 0 and engines[half] != "A"), stop=(t == 3), is_transpose=True,
                    )

        def empty(jt, engines, tile):
            h_b[jt] = tile
            for half in range(2):
                view = turned[jt][half][:].rearrange("p (t j) -> p j t", t=4)
                if engines[half] == "A":
                    nc.scalar.copy(tile[:, half], view)
                else:
                    nc.vector.tensor_tensor(tile[:, half], view, b_rep[:, half], ALU.add)

        def m_tile(tag):
            return sbuf([P, 2, 512], F32, tag)[:]

        def h_tile(tag):
            return sbuf([P, 2, P, 4], BF16, tag)[:]

        def quantize_h(jt, tag, split=False, codes=None):
            if split:
                for a in range(2):
                    h_q[jt, a] = quantize(h_b[jt][:, a].rearrange("p j t -> p (j t)"), P, "%s%d" % (tag, a))
            else:
                into = sbuf([P, 2 * P], U32, codes)[:] if codes else None
                codes, scales = quantize(h_b[jt].rearrange("p a j t -> p (a j t)"), 2 * P, tag, into)
                for a in range(2):
                    h_q[jt, a] = (codes[:, P * a : P * (a + 1)], scales[:, P * a : P * (a + 1)])

        def add_bias_half(jt, half, tag, eng):
            h_b[jt, half] = sbuf([P, 512], BF16, tag)
            eng.tensor_tensor(
                h_b[jt, half][:], damped[jt][:, half], b_rep[:, half].rearrange("p j t -> p (j t)"), ALU.add
            )

        def quantize_half(jt, half, tag, codes):
            h_q[jt, half] = quantize(h_b[jt, half][:], P, tag, sbuf([P, P], U32, codes)[:])

        o_bank = {}

        def scores(jt, name):
            acc = bank(name)
            o_bank[jt] = acc
            for nt in range(4):
                for a in range(2):
                    nc.tensor.matmul_mx(
                        acc[:, P * nt : P * (nt + 1)],
                        lhsT=w3_w[:, a, P * nt : P * (nt + 1)].bitcast(FP8X4),
                        lhsT_scale=w3_s[:, a, P * nt : P * (nt + 1)],
                        rhs=h_q[jt, a][0].bitcast(FP8X4),
                        rhs_scale=h_q[jt, a][1],
                        start=(a == 0),
                        stop=(a == 1),
                    )

        def store(jt, eng, tag):
            result = sbuf([P, 4, P], F32, tag)
            eng(result[:].rearrange("p n j -> p (n j)"), o_bank[jt][:])
            nc.sync.dma_start(out[:, jt * P : (jt + 1) * P].rearrange("(n p) j -> p n j", p=P), result[:])

        def store_pair(jt, tag):
            result = sbuf([P, 4, 2 * P], F32, tag)
            for i in range(2):
                A(result[:, :, P * i : P * (i + 1)], o_bank[jt + i][:].rearrange("p (n j) -> p n j", n=4))
            nc.sync.dma_start(out[:, jt * P : (jt + 2) * P].rearrange("(n p) j -> p n j", p=P), result[:])

        def last_scores(jt, banks, tags):
            accs = [bank(name) for name in banks]
            for a in range(2):
                for nt in range(4):
                    nc.tensor.matmul_mx(
                        accs[nt // 2][:, P * (nt % 2) : P * (nt % 2 + 1)],
                        lhsT=w3_w[:, a, P * nt : P * (nt + 1)].bitcast(FP8X4),
                        lhsT_scale=w3_s[:, a, P * nt : P * (nt + 1)],
                        rhs=h_q[jt, a][0].bitcast(FP8X4),
                        rhs_scale=h_q[jt, a][1],
                        start=(a == 0 and nt % 2 == 0),
                        stop=(a == 1 and nt % 2 == 1),
                    )
            for part, eng in enumerate((A, V)):
                result = sbuf([P, 2, P], F32, tags[part])
                eng(result[:].rearrange("p n j -> p (n j)"), accs[part][:, 0 : 2 * P])
                nc.sync.dma_start(
                    out[256 * part : 256 * (part + 1), jt * P : (jt + 1) * P].rearrange("(n p) j -> p n j", p=P),
                    result[:],
                )

        DA = ("d0", "d1")
        DB = ("d2", "d3")
        E = ("e0", "e1")

        def chunk(lo, a):
            return [(lo, 256, a, t) for t in range(4)]

        load_plane(0, 0)
        b_col = sbuf([P, 2, 4], F32, "b_col")
        nc.sync.dma_start(b_col[:], b.rearrange("(a p t) -> p a t", a=2, t=4))
        for t in range(1, 4):
            load_plane(0, t)
        load_w2(0, 0)
        load_w2(0, 1)
        load_w2(1, 0)
        w1_w = sbuf([P, 2, 2 * H], U8, "w1_w")
        nc.sync.dma_start(w1_w[:].bitcast(I32), w1_words.rearrange("a p n -> p a n").bitcast(I32))
        for t in range(4):
            load_plane(1, t)
        load_w2(1, 1)
        w1_dealt_rows = sbuf([P, H], U8, "w1_dealt_rows")
        nc.gpsimd.tensor_copy(
            w1_dealt_rows[:].rearrange("p (g s m) -> p g s m", g=2, s=4),
            w1_rows[:].rearrange("p (g m s) -> p g s m", g=2, s=4),
        )
        move_scales(v_s, v_rows)
        move_scales(w1_s, w1_dealt_rows)

        b_quads = sbuf([P, 2, 512], F32, "b_quads")
        for a in range(2):
            spread = bank(DB[a])
            for t in range(4):
                nc.tensor.transpose(
                    spread[:, P * t : P * (t + 1)], b_col[:, a, t : t + 1].to_broadcast([P, P]), ident[:]
                )
            nc.scalar.copy(b_quads[:, a, :], spread[:])
        b_rep = sbuf([P, 2, P, 4], F32, "b_rep")
        for a in range(2):
            nc.scalar.copy(b_rep[:, a], b_col[:, a : a + 1, :].to_broadcast([P, P, 4]))

        warm = sbuf([P, 8], F32, "warm")
        nc.scalar.activation(warm[:], b_col[:].rearrange("p a t -> p (a t)"), ACT.Abs_reciprocal_sqrt, bias=1.0)
        OO = ("turn", "o")
        P3 = "VV"
        P4 = "VV"
        P5 = "AA"
        P6 = "AV"
        new_diff(0, 1024, 0, "diffA")
        for t in range(4):
            units = [(0, 512, 0, t), (512, 512, 0, t)]
            pick(units, "cmp%d" % (t % 2))
            subtract(units)
        load_table(0, "plane00")
        load_table(1, "plane01")
        w3_w = sbuf([P, 2, N], U32, "w3_w")
        nc.sync.dma_start(w3_w[:].bitcast(I32), w3_words.rearrange("a p n i -> p a (n i)").bitcast(I32))
        load_scales(w3_s, w3_scales)
        round_w2(0, 0, "w2b0")
        quantize_w2(0, 0)
        round_w2(0, 1, "w2b1")
        quantize_w2(0, 1)
        round_w2(1, 0, "w2b2")
        w1_d = sbuf([P, 2, 2 * H], U8, "w1_d")
        A(
            w1_d[:].bitcast(U16).rearrange("p a (g s m) -> p (a g) s m", g=2, s=4),
            w1_w[:].bitcast(U16).rearrange("p a (g m s) -> p (a g) s m", g=2, s=4),
        )
        round_x(A, 0, 512, 0, "w2raw01")
        round_x(A, 512, 512, 0, "w2raw10")
        new_diff(0, 256, 1, "diffB")
        for t in range(4):
            units = [(0, P, 1, t), (P, P, 1, t)]
            pick(units[0:1], ("cmp0", "xb1", "cmp0", "plane02")[t])
            pick(units[1:2], ("cmp1", "xb0", "cmp1", "root0")[t])
            subtract(units)
        round_x(A, 0, 256, 1, "xb0")
        round_w2(1, 1, "w2b3")
        late = sbuf([P, 3, 512], U32, "plane02")
        quantize_x(0, 512, 0, late[:, 0])
        quantize_w2(1, 0, late[:, 1])
        quantize_x(512, 512, 0, late[:, 2])
        quantize_x(0, 256, 1)
        deviation(0, E, (0,), (0, 1))
        deviation(1, OO, (0,), (0, 1))
        squares(0, "sq0", (0,))
        squares(1, "sq1", (0,))
        new_diff(256, 256, 1, "w2raw11")
        pick(chunk(256, 1)[0:2], "diffB")
        pick(chunk(256, 1)[2:4], "xb0")
        quantize_w2(1, 1)
        deviation(0, E, (1,))
        deviation(1, OO, (1,))
        roots(0, "root0", HALVES[0:1])
        roots(1, "root1", HALVES[0:1])
        squares(0, "sq0", (1,))
        squares(1, "sq1", (1,))
        subtract(chunk(256, 1))
        round_x(GS, 256, 256, 1, "xb1")
        gather_table(0, 256, "diffB")
        pick(chunk(512, 1)[0:2], "xb0")
        response(0, DA)
        roots(0, "root0", HALVES[1:2])
        roots(1, "root1", HALVES[1:2])
        factor(0, "w2raw00")
        factor(1, "w2raw01")
        quantize_x(256, 256, 1)
        response(1, DB)
        deviation(2, E, (0, 1), (0, 1))
        product(0, m_tile("cmp0"))
        deviation(3, OO, (0, 1), (0, 1))
        spread_bias(0, "AA", DA)
        turn_floats(0, "AA")
        pick(chunk(512, 1)[2:4], "root0")
        new_diff(512, 256, 1, "w2raw00")
        subtract(chunk(512, 1))
        round_x(GS, 512, 256, 1, "xb1")
        squares(2, "sq0")
        squares(3, "sq1")
        roots(2, "root2")
        empty(0, "AA", h_tile("hb0"))
        product(1, m_tile("xb0"))
        spread_bias(1, "AA", DB)
        turn_floats(1, "AA")
        gather_table(256, 256, "root0")
        response(2, DA)
        roots(3, "root1")
        factor(2, "w2raw10")
        quantize_x(512, 256, 1)
        direct_deviation(4, E)
        deviation(5, OO, (0, 1), (0, 1))
        quantize_h(0, "hq0")
        pick(chunk(768, 1)[0:2], "w2raw00")
        pick(chunk(768, 1)[2:4], "xb1")
        empty(1, "AA", h_tile("sq1"))
        response(3, DB)
        quantize_h(1, "hq1")
        factor(3, "w2raw11")
        product(2, m_tile("cmp0"))
        spread_bias(2, "AA", DA)
        turn_floats(2, "AA")
        squares(4, "sq0")
        squares(5, "sq2")
        new_diff(768, 256, 1, "root2")
        subtract(chunk(768, 1))
        round_x(GS, 768, 256, 1, "hb0")
        scores(0, "o")
        scores(1, "turn")
        roots(4, "root1")
        empty(2, "AA", h_tile("hb1"))
        roots(5, "root3")
        store_pair(0, "res0")
        factor(4, "w2raw01")
        gather_table(512, 256, "w2raw00")
        product(3, m_tile("sq0"))
        direct_response(4, DA)
        spread_bias(3, "VV", DB)
        turn_floats(3, "VV")
        quantize_x(768, 256, 1, sbuf([P, 256], U32, "w2raw11")[:])
        direct_deviation(6, E)
        direct_deviation(7, OO)
        quantize_h(2, "hq2")
        factor_on_gpsimd(5, "hb0")
        squares(6, "sq1")
        roots(6, "root2", HALVES)
        factor(6, "root3", HALVES)
        squares(7, "sq2")
        gather_table(768, 256, "hb1")
        empty(3, "VV", h_tile("hb2"))
        response(5, DB)
        direct_response(6, E)
        product(4, m_tile("cmp0"))
        quantize_h(3, "hq0", codes="w2raw01")
        scores(2, "d0")
        scores(3, "d1")
        add_bias_half(4, 0, "hb2", nc.gpsimd)
        product(5, m_tile("xb0"))
        spread_bias(5, "AA", DB)
        turn_floats(5, "AA")
        direct_response(7, OO)
        roots(7, "root1", HALVES)
        store_pair(2, "res0")
        factor(7, "w2raw01", HALVES)
        product(6, m_tile("w2raw00"))
        add_bias_half(4, 1, "root3", nc.vector)
        add_bias(6, h_tile("sq0"))
        quantize_half(4, 0, "hq1a", "cmp0")
        quantize_half(4, 1, "hq1b", "hq1")
        scores(4, "e0")
        empty(5, "AA", h_tile("w2raw10"))
        quantize_h(6, "hq0")
        scores(6, "e1")
        last = m_tile("cmp1")
        product(7, last)
        store(4, A, "root2")
        store(6, A, "sq2")
        last_h = h_tile("xb1")
        quantize_h(5, "hq2")
        scores(5, "d0")
        add_bias(7, last_h, (0,))
        add_bias(7, last_h, (1,))
        quantize_h(7, "hq_last", True)
        store(5, A, "sq1")
        last_scores(7, OO, ("xb0", "root0"))
